import numpy as np
import ml_dtypes


def mxq(x, axis, fmt="e4m3"):
    dtype, down = {"e4m3": (ml_dtypes.float8_e4m3fn, 7), "e5m2": (ml_dtypes.float8_e5m2, 14)}[fmt]
    v = np.moveaxis(np.asarray(x, np.float32).astype(ml_dtypes.bfloat16).astype(np.float64), axis, -1)
    blocks = v.reshape(v.shape[:-1] + (-1, 32))
    amax = np.abs(blocks).max(-1, keepdims=True)
    byte = np.maximum(np.where(amax > 0, np.frexp(amax)[1] - 1 + 127, 0) - down, 1)
    scale = np.exp2(byte - 127.0)
    codes = (blocks / scale).astype(np.float32).astype(dtype).astype(np.float64)
    return np.moveaxis((codes * scale).reshape(v.shape), -1, axis)


WIDE = False


def mx_kscale(k):
    if not WIDE:
        return np.ones(k)
    levels = np.array([10, -10, 5, -5, 0])
    if k % 512:
        return np.exp2(np.random.permutation(np.resize(levels, k // 32))).repeat(32)
    a = np.empty((k // 512, 16))
    for p in range(k // 512):
        a[p, :8] = np.random.permutation(np.resize(levels, 8))
        for g in range(8):
            far = levels[np.abs(levels - a[p, g]) >= 10]
            a[p, g + 8] = far[np.random.randint(len(far))]
    return np.exp2(a.ravel()).repeat(32)


def f64(x):
    return np.asarray(x).astype(np.float64)


def striped(idx):
    return np.tile(idx.reshape(-1, 16).T, (8, 1)).astype(np.uint16)


def unstriped(offs):
    return offs[:16].T.reshape(-1).astype(np.int64)


def striped8(idx):
    return np.concatenate([x.reshape(-1, 16).T for x in idx]).astype(np.uint16)


def runs(offs, k):
    lists = np.stack([offs[16 * r : 16 * r + 16].T.reshape(-1) for r in range(8)]).astype(np.int64)
    return lists[np.arange(k) % 512 // 64]


def pack_weight(w):
    k, n = w.shape
    w = f64(np.asarray(w, np.float32).astype(ml_dtypes.bfloat16)).reshape(k // 32, 32, n)
    amax = np.abs(w).max(1)
    byte = np.clip(np.where(amax > 0, np.frexp(amax)[1] - 1 + 127 - 7, 1), 1, 254)
    scaled = (w * np.exp2(127.0 - byte)[:, None, :]).reshape(k, n).astype(np.float32)
    words = np.ascontiguousarray(scaled.reshape(k // 512, 128, 4, n).transpose(0, 1, 3, 2)).astype(ml_dtypes.float8_e4m3fn).view(np.uint8)
    return words, np.ascontiguousarray(byte.astype(np.uint8).reshape(k // 512, 16, n))


def unpack_weight(words, scales):
    g, p, n, _ = words.shape
    vals = np.ascontiguousarray(words).view(ml_dtypes.float8_e4m3fn).astype(np.float64) * np.repeat(np.exp2(scales.astype(np.float64) - 127.0), 8, axis=1)[..., None]
    return vals.transpose(0, 1, 3, 2).reshape(g * 512, n)

def planes(y):
    n, m = y.shape
    v = y.astype(np.float32).astype(ml_dtypes.bfloat16).astype(np.float64).reshape(n // 32, 32, m)
    top = np.abs(v).max(1)
    byte = np.clip(np.where(top > 0, np.frexp(top)[1] - 1 + 127 - 7, 1), 1, 254)
    codes = (v * np.exp2(127.0 - byte)[:, None, :]).reshape(n, m).astype(np.float32).astype(ml_dtypes.float8_e4m3fn).view(np.uint8)
    words = codes.reshape(n // 512, 128, 4, m).transpose(0, 1, 3, 2)
    return np.ascontiguousarray(words), np.ascontiguousarray(byte.astype(np.uint8).reshape(n // 512, 16, m))


K, T, S, V, N = 512, 2048, 512, 256, 512


def setup_inputs():
    n = np.random.standard_normal
    s = mx_kscale(K)[:, None]
    packed_xT = pack_weight(n((K, T)) * s)
    return {
        "x_words": packed_xT[0],
        "x_scales": packed_xT[1],
        "w1": (n((K, N)) / np.sqrt(K) / s).astype(np.float32),
        "w2": (n((K, N)) / np.sqrt(K) / s).astype(np.float32),
        "sh": np.repeat(np.random.uniform(0.2, 0.8, (8, V)), 64, axis=0).astype(np.float32),
        "offs": striped(np.random.permutation(T)[:S]),
        "acc_l": striped8(np.stack([np.random.permutation(S)[:V] for _ in range(8)])),
    }


def reference(x_words, x_scales, w1, w2, sh, offs, acc_l):
    xq = unpack_weight(x_words, x_scales)[:, unstriped(offs)]
    y = mxq(f64(w1), 0, "e4m3").T @ xq
    yt = y[np.arange(N)[:, None], runs(acc_l, N)]
    e = mxq(f64(w2), 0, "e4m3").T @ xq
    q = yt + f64(sh) * (e[np.arange(N)[:, None], runs(acc_l, N)] - yt)
    out = y.copy()
    out[np.arange(N)[:, None], runs(acc_l, N)] = q
    return (out,) + planes(out)

@@ -1,0 +1,141 @@
+from contextlib import ExitStack
+
+import concourse.mybir as mybir
+
+K, T, S, V, N = 512, 2048, 512, 256, 512
+FLOPS = 2 * 2 * K * N * S
+
+F32 = mybir.dt.float32
+BF16 = mybir.dt.bfloat16
+I32 = mybir.dt.int32
+U32 = mybir.dt.uint32
+U16 = mybir.dt.uint16
+U8 = mybir.dt.uint8
+FP8X4 = mybir.dt.float8_e4m3fn_x4
+MULT = mybir.AluOpType.mult
+ADD = mybir.AluOpType.add
+P = 128
+PACK = 4
+
+
+def tile_picked_specacc_none_po_kernel(tc, x_words, x_scales, w1, w2, sh, offs, acc_l, out_0, out_1, out_2):
+    nc = tc.nc
+    with ExitStack() as ctx:
+        keep = ctx.enter_context(tc.tile_pool(name="keep", bufs=1))
+        psum = ctx.enter_context(tc.psum_pool(name="psum", bufs=1))
+        HALF = N // 2
+
+        scale_table = keep.tile([P, T], U8, name="scale_table")
+        nc.vector.memset(scale_table[:, : T // 2].bitcast(I32), 0)
+        nc.gpsimd.memset(scale_table[:, T // 2 :].bitcast(I32), 0)
+
+        raw1 = keep.tile([P, PACK, N], F32, name="raw1")
+        nc.sync.dma_start(raw1[:], w1.rearrange("(p j) c -> p j c", j=PACK))
+        picks = keep.tile([P, S // 16], U16, name="picks")
+        nc.sync.dma_start(picks[:], offs)
+        for q in range(4):
+            nc.sync.dma_start(scale_table[32 * q : 32 * q + 4, :].bitcast(I32), x_scales[0, 4 * q : 4 * q + 4, :].bitcast(I32))
+        word_table = keep.tile([P, T], U32, name="word_table")
+        nc.sync.dma_start(word_table[:].bitcast(I32), x_words[0].rearrange("p n t -> p (n t)").bitcast(I32))
+        accepted = keep.tile([P, V // 16], U16, name="accepted")
+        nc.sync.dma_start(accepted[:], acc_l)
+        share = keep.tile([P, V], F32, name="share")
+        nc.sync.dma_start(share[:], sh.rearrange("(p t) v -> p t v", t=PACK)[:, 0, :])
+        raw2 = []
+        for h in range(2):
+            raw2.append(keep.tile([P, PACK, HALF], F32, name=f"raw2_{h}", align_bytes=64))
+            nc.sync.dma_start(raw2[h][:], w2.rearrange("(p j) c -> p j c", j=PACK)[:, :, h * HALF : (h + 1) * HALF])
+
+        def cast(grouped, raw, first, c0, c1, copy):
+            copy(grouped[:, :, (first + c0) // PACK : (first + c1) // PACK, :].rearrange("p t m j -> p m j t"),
+                 raw[:, :, c0:c1].rearrange("p j (m t) -> p m j t", t=PACK))
+
+        def quantise(grouped, name):
+            planes = {}
+            for u in range(2):
+                codes = keep.tile([P, 2 * P], U32, name=f"codes_{name}{u}", align_bytes=64)
+                scales = keep.tile([P, 2 * P], U8, name=f"scales_{name}{u}", align_bytes=64)
+                nc.vector.quantize_mx(out=codes[:].bitcast(FP8X4), scales=scales[:],
+                                      in_=grouped[:, 2 * u : 2 * u + 2, :, :].rearrange("p t m j -> p (t m j)"))
+                for i in range(2):
+                    planes[2 * u + i] = (codes[:, i * P : (i + 1) * P], scales[:, i * P : (i + 1) * P])
+            return planes
+
+        def product(weights, bank, c0, c1):
+            codes, scales = weights
+            nc.tensor.matmul_mx(out=bank, lhsT=codes.bitcast(FP8X4), lhsT_scale=scales,
+                                rhs=x_codes[:, c0:c1].bitcast(FP8X4), rhs_scale=x_scale[:, c0:c1], start=True, stop=True)
+
+        ORDER = (0, 2, 3, 1)
+        x_scale = keep.tile([P, S], U8, name="x_scale", align_bytes=64)
+        nc.vector.tensor_copy(x_scale[:], scale_table[:].indirect(picks[:]))
+        grouped1 = keep.tile([P, PACK, P, PACK], BF16, name="grouped1", align_bytes=64)
+        cast(grouped1, raw1, 0, 0, 176, nc.vector.tensor_copy)
+        cast(grouped1, raw1, 0, 176, N, nc.scalar.copy)
+        q1 = quantise(grouped1, "w1")
+        x_codes = keep.tile([P, S], U32, name="x_codes", align_bytes=64)
+        for h in range(2):
+            nc.vector.tensor_copy(x_codes[:, h * 256 : (h + 1) * 256], word_table[:].indirect(picks[:, h * 16 : (h + 1) * 16]))
+
+        y = {}
+        first = ORDER[0]
+        y[first] = keep.tile([P, S], F32, name=f"y{first}")
+        for h in range(2):
+            bank = psum.tile([P, 256], F32, name=f"bank{h}")
+            product(q1[first], bank[:], h * 256, (h + 1) * 256)
+            copy = nc.scalar.copy if h == 0 else nc.vector.tensor_copy
+            copy(y[first][:, h * 256 : (h + 1) * 256], bank[:])
+        rest = keep.tile([P, V], F32, name="rest")
+        nc.scalar.activation(rest[:], share[:], mybir.ActivationFunctionType.Copy, bias=1.0, scale=-1.0)
+
+        grouped2 = keep.tile([P, PACK, P, PACK], BF16, name="grouped2", align_bytes=64)
+        cast(grouped2, raw2[0], 0, 0, HALF, nc.scalar.copy)
+        cast(grouped2, raw2[1], HALF, 0, 160, nc.vector.tensor_copy)
+        cast(grouped2, raw2[1], HALF, 160, HALF, nc.scalar.copy)
+        q2 = quantise(grouped2, "w2")
+
+        e = {}
+        def draft(t, b):
+            bank = psum.tile([P, S], F32, name=f"bank{b}")
+            product(q2[t], bank[:], 0, S)
+            e[t] = keep.tile([P, S], F32, name=f"e{t}")
+            nc.scalar.copy(e[t][:], bank[:])
+        def target(t, b, slot):
+            bank = psum.tile([P, S], F32, name=f"bank{b}")
+            product(q1[t], bank[:], 0, S)
+            y[t] = keep.tile([P, S], F32, name=slot, align_bytes=64)
+            nc.scalar.copy(y[t][:], bank[:])
+        target(ORDER[1], 2, "y_second")
+        target(ORDER[2], 3, "raw2_1")
+        draft(ORDER[0], 5)
+        target(ORDER[3], 4, "grouped2")
+        for i, t in enumerate(ORDER[1:]):
+            draft(t, (6 + i) % 8)
+
+        woven = keep.tile([P, S, PACK], BF16, name="woven", align_bytes=64)
+        out_rows = out_0.rearrange("(p t) c -> p t c", t=PACK)
+        SPLIT = 336
+        for t in ORDER:
+            ya = keep.tile([P, V], F32, name=f"ya{t}")
+            nc.vector.tensor_tensor(ya[:], y[t][:].indirect(accepted[:]), rest[:], MULT)
+            ea = keep.tile([P, V], F32, name=f"ea{t}" if t != ORDER[-1] else f"y{ORDER[0]}")
+            nc.vector.tensor_tensor(ea[:], e[t][:].indirect(accepted[:]), share[:], MULT)
+            nc.vector.tensor_tensor(y[t][:].indirect(accepted[:]), ya[:], ea[:], ADD)
+            nc.sync.dma_start(out_rows[:, t, :], y[t][:])
+            if t != ORDER[-1]:
+                nc.scalar.copy(woven[:, :, t], y[t][:])
+            else:
+                nc.vector.tensor_copy(woven[:, :256, t], y[t][:, :256])
+                nc.vector.tensor_copy(woven[:, 256:SPLIT, t], y[t][:, 256:SPLIT])
+                nc.scalar.copy(woven[:, SPLIT:, t], y[t][:, SPLIT:])
+
+        out_scales = keep.tile([P, S], U8, name="out_scales", align_bytes=64)
+        out_words = out_1[0].rearrange("p c t -> p (c t)").bitcast(I32)
+        for h in range(2):
+            cols = slice(256 * h, 256 * (h + 1))
+            out_codes = keep.tile([P, 256], U32, name=f"out_codes{h}", align_bytes=64)
+            nc.vector.quantize_mx(out=out_codes[:].bitcast(FP8X4), scales=out_scales[:, cols], in_=woven[:, cols, :].rearrange("p c t -> p (c t)"))
+            nc.sync.dma_start(out_words[:, cols], out_codes[:].bitcast(I32))
+        for q in range(4):
+            queue = nc.scalar if q % 2 == 0 else nc.sync
+            queue.dma_start(out_2[0, 4 * q : 4 * q + 4, :].bitcast(I32), out_scales[32 * q : 32 * q + 4, :].bitcast(I32))

@@ -14,128 +14,183 @@ U8 = mybir.dt.uint8
 FP8X4 = mybir.dt.float8_e4m3fn_x4
 MULT = mybir.AluOpType.mult
 ADD = mybir.AluOpType.add
+COPY = mybir.ActivationFunctionType.Copy
+
 P = 128
 PACK = 4
+QUADRANT = 32
+LIST_ROWS = 16
+PLANE_BYTES = 4 * S
+
+ORDER = (0, 2, 3, 1)
+
+W2_VECTOR = 176
+W1_FIRST = 352
+W1_VECTOR = 224
+FIRST_PLANE_PIECES = ((0, 0, 256), (1, 256, 384), (7, 384, 512))
+LAST_VECTOR_CUT, LAST_VECTOR = 128, 288
+OUT_PIECES = ((0, 128), (128, 256), (256, 512))
 
 
-def tile_picked_specacc_none_po_kernel(tc, x_words, x_scales, w1, w2, sh, offs, acc_l, out_0, out_1, out_2):
+def tile_picked_specacc_none_po_kernel(
+    tc, x_words, x_scales, w1, w2, sh, offs, acc_l, out_0, out_1, out_2
+):
     nc = tc.nc
     with ExitStack() as ctx:
         keep = ctx.enter_context(tc.tile_pool(name="keep", bufs=1))
         psum = ctx.enter_context(tc.psum_pool(name="psum", bufs=1))
-        HALF = N // 2
+        stage = ctx.enter_context(tc.tile_pool(name="stage", bufs=1))
 
         scale_table = keep.tile([P, T], U8, name="scale_table")
         nc.vector.memset(scale_table[:, : T // 2].bitcast(I32), 0)
         nc.gpsimd.memset(scale_table[:, T // 2 :].bitcast(I32), 0)
 
-        raw1 = keep.tile([P, PACK, N], F32, name="raw1")
-        nc.sync.dma_start(raw1[:], w1.rearrange("(p j) c -> p j c", j=PACK))
-        picks = keep.tile([P, S // 16], U16, name="picks")
+        raw2 = keep.tile([P, PACK, N], F32, name="raw2")
+        nc.sync.dma_start(raw2[:], w2.rearrange("(p j) c -> p j c", j=PACK))
+        picks = keep.tile([P, S // LIST_ROWS], U16, name="picks")
         nc.sync.dma_start(picks[:], offs)
-        for q in range(4):
-            nc.sync.dma_start(scale_table[32 * q : 32 * q + 4, :].bitcast(I32), x_scales[0, 4 * q : 4 * q + 4, :].bitcast(I32))
+        for r in range(PACK):
+            nc.sync.dma_start(scale_table[r:P:QUADRANT, :].bitcast(I32), x_scales[0, r:16:PACK, :].bitcast(I32))
         word_table = keep.tile([P, T], U32, name="word_table")
         nc.sync.dma_start(word_table[:].bitcast(I32), x_words[0].rearrange("p n t -> p (n t)").bitcast(I32))
-        accepted = keep.tile([P, V // 16], U16, name="accepted")
+        raw1_first = stage.tile([P, PACK, W1_FIRST], F32, name="raw1_first", offset=0)
+        raw1_second = keep.tile([P, PACK, N - W1_FIRST], F32, name="raw1_second")
+        w1_rows = w1.rearrange("(p j) c -> p j c", j=PACK)
+        nc.sync.dma_start(raw1_first[:], w1_rows[:, :, :W1_FIRST])
+        accepted = keep.tile([P, V // LIST_ROWS], U16, name="accepted")
         nc.sync.dma_start(accepted[:], acc_l)
+        nc.sync.dma_start(raw1_second[:], w1_rows[:, :, W1_FIRST:])
         share = keep.tile([P, V], F32, name="share")
         nc.sync.dma_start(share[:], sh.rearrange("(p t) v -> p t v", t=PACK)[:, 0, :])
-        raw2 = []
-        for h in range(2):
-            raw2.append(keep.tile([P, PACK, HALF], F32, name=f"raw2_{h}", align_bytes=64))
-            nc.sync.dma_start(raw2[h][:], w2.rearrange("(p j) c -> p j c", j=PACK)[:, :, h * HALF : (h + 1) * HALF])
 
-        def cast(grouped, raw, first, c0, c1, copy):
-            copy(grouped[:, :, (first + c0) // PACK : (first + c1) // PACK, :].rearrange("p t m j -> p m j t"),
-                 raw[:, :, c0:c1].rearrange("p j (m t) -> p m j t", t=PACK))
+        def round_weights(grouped, raw, base, c0, c1, copy):
+            copy(
+                grouped[:, :, (base + c0) // PACK : (base + c1) // PACK, :].rearrange("p t m j -> p m j t"),
+                raw[:, :, c0:c1].rearrange("p j (m t) -> p m j t", t=PACK),
+            )
 
-        def quantise(grouped, name):
-            planes = {}
-            for u in range(2):
-                codes = keep.tile([P, 2 * P], U32, name=f"codes_{name}{u}", align_bytes=64)
-                scales = keep.tile([P, 2 * P], U8, name=f"scales_{name}{u}", align_bytes=64)
-                nc.vector.quantize_mx(out=codes[:].bitcast(FP8X4), scales=scales[:],
-                                      in_=grouped[:, 2 * u : 2 * u + 2, :, :].rearrange("p t m j -> p (t m j)"))
+        def quantise_weights(grouped, name):
+            operands = {}
+            for pair in range(2):
+                codes = keep.tile([P, 2 * P], U32, name=f"codes_{name}{pair}", align_bytes=64)
+                scales = keep.tile([P, 2 * P], U8, name=f"scales_{name}{pair}", align_bytes=64)
+                nc.vector.quantize_mx(
+                    out=codes[:].bitcast(FP8X4),
+                    scales=scales[:],
+                    in_=grouped[:, 2 * pair : 2 * pair + 2, :, :].rearrange("p t m j -> p (t m j)"),
+                )
                 for i in range(2):
-                    planes[2 * u + i] = (codes[:, i * P : (i + 1) * P], scales[:, i * P : (i + 1) * P])
-            return planes
+                    operands[2 * pair + i] = (codes[:, i * P : (i + 1) * P], scales[:, i * P : (i + 1) * P])
+            return operands
 
-        def product(weights, bank, c0, c1):
-            codes, scales = weights
-            nc.tensor.matmul_mx(out=bank, lhsT=codes.bitcast(FP8X4), lhsT_scale=scales,
-                                rhs=x_codes[:, c0:c1].bitcast(FP8X4), rhs_scale=x_scale[:, c0:c1], start=True, stop=True)
+        def product(operand, dest, bank_no, c0, c1):
+            codes, scales = operand
+            bank = psum.tile([P, c1 - c0], F32, name=f"bank{bank_no}")
+            nc.tensor.matmul_mx(
+                out=bank[:],
+                lhsT=codes.bitcast(FP8X4),
+                lhsT_scale=scales,
+                rhs=x_codes[:, c0:c1].bitcast(FP8X4),
+                rhs_scale=x_scale[:, c0:c1],
+                start=True,
+                stop=True,
+            )
+            nc.scalar.copy(dest[:, c0:c1], bank[:])
 
-        ORDER = (0, 2, 3, 1)
         x_scale = keep.tile([P, S], U8, name="x_scale", align_bytes=64)
         nc.vector.tensor_copy(x_scale[:], scale_table[:].indirect(picks[:]))
-        grouped1 = keep.tile([P, PACK, P, PACK], BF16, name="grouped1", align_bytes=64)
-        cast(grouped1, raw1, 0, 0, 176, nc.vector.tensor_copy)
-        cast(grouped1, raw1, 0, 176, N, nc.scalar.copy)
-        q1 = quantise(grouped1, "w1")
+        grouped2 = keep.tile([P, PACK, P, PACK], BF16, name="grouped2", align_bytes=64)
+        round_weights(grouped2, raw2, 0, 0, W2_VECTOR, nc.vector.tensor_copy)
+        round_weights(grouped2, raw2, 0, W2_VECTOR, N, nc.scalar.copy)
+        draft_weights = quantise_weights(grouped2, "w2")
         x_codes = keep.tile([P, S], U32, name="x_codes", align_bytes=64)
+        half, half_list = S // 2, S // 2 // LIST_ROWS
         for h in range(2):
-            nc.vector.tensor_copy(x_codes[:, h * 256 : (h + 1) * 256], word_table[:].indirect(picks[:, h * 16 : (h + 1) * 16]))
+            offsets = picks[:, h * half_list : (h + 1) * half_list]
+            nc.vector.tensor_copy(x_codes[:, h * half : (h + 1) * half], word_table[:].indirect(offsets))
+
+        grouped1 = keep.tile([P, PACK, P, PACK], BF16, name="grouped1", align_bytes=64)
+        round_weights(grouped1, raw1_first, 0, 0, W1_VECTOR, nc.vector.tensor_copy)
+        round_weights(grouped1, raw1_second, W1_FIRST, 0, N - W1_FIRST, nc.vector.tensor_copy)
+
+        first, second, third, last = ORDER
+        e = {first: keep.tile([P, S], F32, name="e_first")}
+        for i, t in enumerate(ORDER[1:]):
+            e[t] = stage.tile([P, S], F32, name=f"e{t}", offset=PLANE_BYTES * i)
+        for bank_no, c0, c1 in FIRST_PLANE_PIECES:
+            product(draft_weights[first], e[first], bank_no, c0, c1)
+            if c0 == 0:
+                round_weights(grouped1, raw1_first, 0, W1_VECTOR, W1_FIRST, nc.scalar.copy)
+
+        draft_part = {}
+
+        def look_up_draft(t, slot):
+            draft_part[t] = keep.tile([P, V], F32, name=slot)
+            nc.vector.tensor_tensor(draft_part[t][:], e[t][:].indirect(accepted[:]), share[:], MULT)
 
         y = {}
-        first = ORDER[0]
-        y[first] = keep.tile([P, S], F32, name=f"y{first}")
-        for h in range(2):
-            bank = psum.tile([P, 256], F32, name=f"bank{h}")
-            product(q1[first], bank[:], h * 256, (h + 1) * 256)
-            copy = nc.scalar.copy if h == 0 else nc.vector.tensor_copy
-            copy(y[first][:, h * 256 : (h + 1) * 256], bank[:])
-        rest = keep.tile([P, V], F32, name="rest")
-        nc.scalar.activation(rest[:], share[:], mybir.ActivationFunctionType.Copy, bias=1.0, scale=-1.0)
 
-        grouped2 = keep.tile([P, PACK, P, PACK], BF16, name="grouped2", align_bytes=64)
-        cast(grouped2, raw2[0], 0, 0, HALF, nc.scalar.copy)
-        cast(grouped2, raw2[1], HALF, 0, 160, nc.vector.tensor_copy)
-        cast(grouped2, raw2[1], HALF, 160, HALF, nc.scalar.copy)
-        q2 = quantise(grouped2, "w2")
-
-        e = {}
-        def draft(t, b):
-            bank = psum.tile([P, S], F32, name=f"bank{b}")
-            product(q2[t], bank[:], 0, S)
-            e[t] = keep.tile([P, S], F32, name=f"e{t}")
-            nc.scalar.copy(e[t][:], bank[:])
-        def target(t, b, slot):
-            bank = psum.tile([P, S], F32, name=f"bank{b}")
-            product(q1[t], bank[:], 0, S)
+        def target_plane(t, bank_no, slot):
             y[t] = keep.tile([P, S], F32, name=slot, align_bytes=64)
-            nc.scalar.copy(y[t][:], bank[:])
-        target(ORDER[1], 2, "y_second")
-        target(ORDER[2], 3, "raw2_1")
-        draft(ORDER[0], 5)
-        target(ORDER[3], 4, "grouped2")
-        for i, t in enumerate(ORDER[1:]):
-            draft(t, (6 + i) % 8)
+            product(target_weights[t], y[t], bank_no, 0, S)
+
+        product(draft_weights[second], e[second], 2, 0, S)
+        look_up_draft(first, "raw1_second")
+        target_weights = quantise_weights(grouped1, "w1")
+        look_up_draft(second, "draft_second")
+        product(draft_weights[third], e[third], 3, 0, S)
+        rest = keep.tile([P, V], F32, name="rest")
+        nc.scalar.activation(rest[:], share[:], COPY, bias=1.0, scale=-1.0)
+        target_plane(first, 5, "y_first")
+        product(draft_weights[last], e[last], 4, 0, S)
+        target_plane(second, 6, "y_second")
+        target_plane(third, 7, "y_third")
+        look_up_draft(third, "draft_third")
+        look_up_draft(last, "draft_last")
+
+        target_part = {}
+
+        def look_up_target(t):
+            target_part[t] = keep.tile([P, V], F32, name=f"target_part{t}", align_bytes=64)
+            nc.vector.tensor_tensor(target_part[t][:], y[t][:].indirect(accepted[:]), rest[:], MULT)
 
         woven = keep.tile([P, S, PACK], BF16, name="woven", align_bytes=64)
         out_rows = out_0.rearrange("(p t) c -> p t c", t=PACK)
-        SPLIT = 336
-        for t in ORDER:
-            ya = keep.tile([P, V], F32, name=f"ya{t}")
-            nc.vector.tensor_tensor(ya[:], y[t][:].indirect(accepted[:]), rest[:], MULT)
-            ea = keep.tile([P, V], F32, name=f"ea{t}" if t != ORDER[-1] else f"y{ORDER[0]}")
-            nc.vector.tensor_tensor(ea[:], e[t][:].indirect(accepted[:]), share[:], MULT)
-            nc.vector.tensor_tensor(y[t][:].indirect(accepted[:]), ya[:], ea[:], ADD)
+
+        def put_back(t):
+            nc.vector.tensor_tensor(y[t][:].indirect(accepted[:]), target_part[t][:], draft_part[t][:], ADD)
             nc.sync.dma_start(out_rows[:, t, :], y[t][:])
-            if t != ORDER[-1]:
-                nc.scalar.copy(woven[:, :, t], y[t][:])
-            else:
-                nc.vector.tensor_copy(woven[:, :256, t], y[t][:, :256])
-                nc.vector.tensor_copy(woven[:, 256:SPLIT, t], y[t][:, 256:SPLIT])
-                nc.scalar.copy(woven[:, SPLIT:, t], y[t][:, SPLIT:])
+
+        look_up_target(first)
+        look_up_target(second)
+        put_back(first)
+        nc.scalar.copy(woven[:, :, first], y[first][:])
+        target_plane(last, 0, f"target_part{first}")
+        look_up_target(third)
+        put_back(second)
+        nc.scalar.copy(woven[:, :, second], y[second][:])
+        look_up_target(last)
+        put_back(third)
+        nc.scalar.copy(woven[:, :, third], y[third][:])
+        put_back(last)
+        nc.vector.tensor_copy(woven[:, :LAST_VECTOR_CUT, last], y[last][:, :LAST_VECTOR_CUT])
+        nc.vector.tensor_copy(woven[:, LAST_VECTOR_CUT:LAST_VECTOR, last], y[last][:, LAST_VECTOR_CUT:LAST_VECTOR])
+        nc.scalar.copy(woven[:, LAST_VECTOR:, last], y[last][:, LAST_VECTOR:])
 
         out_scales = keep.tile([P, S], U8, name="out_scales", align_bytes=64)
         out_words = out_1[0].rearrange("p c t -> p (c t)").bitcast(I32)
-        for h in range(2):
-            cols = slice(256 * h, 256 * (h + 1))
-            out_codes = keep.tile([P, 256], U32, name=f"out_codes{h}", align_bytes=64)
-            nc.vector.quantize_mx(out=out_codes[:].bitcast(FP8X4), scales=out_scales[:, cols], in_=woven[:, cols, :].rearrange("p c t -> p (c t)"))
-            nc.sync.dma_start(out_words[:, cols], out_codes[:].bitcast(I32))
-        for q in range(4):
+        out_codes = keep.tile([P, S], U32, name="out_codes", align_bytes=64)
+        for c0, c1 in OUT_PIECES:
+            nc.vector.quantize_mx(
+                out=out_codes[:, c0:c1].bitcast(FP8X4),
+                scales=out_scales[:, c0:c1],
+                in_=woven[:, c0:c1, :].rearrange("p c t -> p (c t)"),
+            )
+            if c1 % half == 0:
+                nc.sync.dma_start(out_words[:, c1 - half : c1], out_codes[:, c1 - half : c1].bitcast(I32))
+        for q in range(P // QUADRANT):
             queue = nc.scalar if q % 2 == 0 else nc.sync
-            queue.dma_start(out_2[0, 4 * q : 4 * q + 4, :].bitcast(I32), out_scales[32 * q : 32 * q + 4, :].bitcast(I32))
+            queue.dma_start(
+                out_2[0, PACK * q : PACK * (q + 1), :].bitcast(I32),
+                out_scales[QUADRANT * q : QUADRANT * q + PACK, :].bitcast(I32),
+            )

@@ -25,8 +25,7 @@ PLANE_BYTES = 4 * S
 ORDER = (0, 2, 3, 1)
 
 W2_VECTOR = 176
-W1_FIRST = 352
-W1_VECTOR = 224
+W1_CUTS = (0, 128, 384, 512)
 FIRST_PLANE_PIECES = ((0, 0, 256), (1, 256, 384), (7, 384, 512))
 LAST_VECTOR_CUT, LAST_VECTOR = 128, 288
 OUT_PIECES = ((0, 128), (128, 256), (256, 512))
@@ -53,13 +52,16 @@ def tile_picked_specacc_none_po_kernel(
             nc.sync.dma_start(scale_table[r:P:QUADRANT, :].bitcast(I32), x_scales[0, r:16:PACK, :].bitcast(I32))
         word_table = keep.tile([P, T], U32, name="word_table")
         nc.sync.dma_start(word_table[:].bitcast(I32), x_words[0].rearrange("p n t -> p (n t)").bitcast(I32))
-        raw1_first = stage.tile([P, PACK, W1_FIRST], F32, name="raw1_first", offset=0)
-        raw1_second = keep.tile([P, PACK, N - W1_FIRST], F32, name="raw1_second")
+        cut0, cut1, cut2, cut3 = W1_CUTS
+        raw1_first = stage.tile([P, PACK, cut1 - cut0], F32, name="raw1_first", offset=PLANE_BYTES // 2)
+        raw1_second = stage.tile([P, PACK, cut2 - cut1], F32, name="raw1_second", offset=2 * PLANE_BYTES)
+        raw1_third = keep.tile([P, PACK, cut3 - cut2], F32, name="raw1_third")
         w1_rows = w1.rearrange("(p j) c -> p j c", j=PACK)
-        nc.sync.dma_start(raw1_first[:], w1_rows[:, :, :W1_FIRST])
+        nc.sync.dma_start(raw1_first[:], w1_rows[:, :, cut0:cut1])
+        nc.sync.dma_start(raw1_second[:], w1_rows[:, :, cut1:cut2])
         accepted = keep.tile([P, V // LIST_ROWS], U16, name="accepted")
         nc.sync.dma_start(accepted[:], acc_l)
-        nc.sync.dma_start(raw1_second[:], w1_rows[:, :, W1_FIRST:])
+        nc.sync.dma_start(raw1_third[:], w1_rows[:, :, cut2:cut3])
         share = keep.tile([P, V], F32, name="share")
         nc.sync.dma_start(share[:], sh.rearrange("(p t) v -> p t v", t=PACK)[:, 0, :])
 
@@ -110,8 +112,9 @@ def tile_picked_specacc_none_po_kernel(
             nc.vector.tensor_copy(x_codes[:, h * half : (h + 1) * half], word_table[:].indirect(offsets))
 
         grouped1 = keep.tile([P, PACK, P, PACK], BF16, name="grouped1", align_bytes=64)
-        round_weights(grouped1, raw1_first, 0, 0, W1_VECTOR, nc.vector.tensor_copy)
-        round_weights(grouped1, raw1_second, W1_FIRST, 0, N - W1_FIRST, nc.vector.tensor_copy)
+        round_weights(grouped1, raw1_first, cut0, 0, cut1 - cut0, nc.scalar.copy)
+        round_weights(grouped1, raw1_second, cut1, 0, cut2 - cut1, nc.vector.tensor_copy)
+        round_weights(grouped1, raw1_third, cut2, 0, cut3 - cut2, nc.vector.tensor_copy)
 
         first, second, third, last = ORDER
         e = {first: keep.tile([P, S], F32, name="e_first")}
@@ -119,8 +122,6 @@ def tile_picked_specacc_none_po_kernel(
             e[t] = stage.tile([P, S], F32, name=f"e{t}", offset=PLANE_BYTES * i)
         for bank_no, c0, c1 in FIRST_PLANE_PIECES:
             product(draft_weights[first], e[first], bank_no, c0, c1)
-            if c0 == 0:
-                round_weights(grouped1, raw1_first, 0, W1_VECTOR, W1_FIRST, nc.scalar.copy)
 
         draft_part = {}
 
@@ -135,7 +136,7 @@ def tile_picked_specacc_none_po_kernel(
             product(target_weights[t], y[t], bank_no, 0, S)
 
         product(draft_weights[second], e[second], 2, 0, S)
-        look_up_draft(first, "raw1_second")
+        look_up_draft(first, "raw1_third")
         target_weights = quantise_weights(grouped1, "w1")
         look_up_draft(second, "draft_second")
         product(draft_weights[third], e[third], 3, 0, S)

@@ -25,8 +25,9 @@ PLANE_BYTES = 4 * S
 ORDER = (0, 2, 3, 1)
 
 W2_VECTOR = 176
-W1_CUTS = (0, 128, 384, 512)
+W1_VECTOR = 344
 FIRST_PLANE_PIECES = ((0, 0, 256), (1, 256, 384), (7, 384, 512))
+TARGET_BANKS = (5, 6, 7, 0)
 LAST_VECTOR_CUT, LAST_VECTOR = 128, 288
 OUT_PIECES = ((0, 128), (128, 256), (256, 512))
 
@@ -52,16 +53,10 @@ def tile_picked_specacc_none_po_kernel(
             nc.sync.dma_start(scale_table[r:P:QUADRANT, :].bitcast(I32), x_scales[0, r:16:PACK, :].bitcast(I32))
         word_table = keep.tile([P, T], U32, name="word_table")
         nc.sync.dma_start(word_table[:].bitcast(I32), x_words[0].rearrange("p n t -> p (n t)").bitcast(I32))
-        cut0, cut1, cut2, cut3 = W1_CUTS
-        raw1_first = stage.tile([P, PACK, cut1 - cut0], F32, name="raw1_first", offset=PLANE_BYTES // 2)
-        raw1_second = stage.tile([P, PACK, cut2 - cut1], F32, name="raw1_second", offset=2 * PLANE_BYTES)
-        raw1_third = keep.tile([P, PACK, cut3 - cut2], F32, name="raw1_third")
-        w1_rows = w1.rearrange("(p j) c -> p j c", j=PACK)
-        nc.sync.dma_start(raw1_first[:], w1_rows[:, :, cut0:cut1])
-        nc.sync.dma_start(raw1_second[:], w1_rows[:, :, cut1:cut2])
+        raw1 = stage.tile([P, PACK, N], F32, name="raw1", offset=0)
+        nc.sync.dma_start(raw1[:], w1.rearrange("(p j) c -> p j c", j=PACK))
         accepted = keep.tile([P, V // LIST_ROWS], U16, name="accepted")
         nc.sync.dma_start(accepted[:], acc_l)
-        nc.sync.dma_start(raw1_third[:], w1_rows[:, :, cut2:cut3])
         share = keep.tile([P, V], F32, name="share")
         nc.sync.dma_start(share[:], sh.rearrange("(p t) v -> p t v", t=PACK)[:, 0, :])
 
@@ -98,6 +93,7 @@ def tile_picked_specacc_none_po_kernel(
                 stop=True,
             )
             nc.scalar.copy(dest[:, c0:c1], bank[:])
+            return bank
 
         x_scale = keep.tile([P, S], U8, name="x_scale", align_bytes=64)
         nc.vector.tensor_copy(x_scale[:], scale_table[:].indirect(picks[:]))
@@ -112,9 +108,8 @@ def tile_picked_specacc_none_po_kernel(
             nc.vector.tensor_copy(x_codes[:, h * half : (h + 1) * half], word_table[:].indirect(offsets))
 
         grouped1 = keep.tile([P, PACK, P, PACK], BF16, name="grouped1", align_bytes=64)
-        round_weights(grouped1, raw1_first, cut0, 0, cut1 - cut0, nc.scalar.copy)
-        round_weights(grouped1, raw1_second, cut1, 0, cut2 - cut1, nc.vector.tensor_copy)
-        round_weights(grouped1, raw1_third, cut2, 0, cut3 - cut2, nc.vector.tensor_copy)
+        round_weights(grouped1, raw1, 0, 0, W1_VECTOR, nc.vector.tensor_copy)
+        round_weights(grouped1, raw1, 0, W1_VECTOR, N, nc.scalar.copy)
 
         first, second, third, last = ORDER
         e = {first: keep.tile([P, S], F32, name="e_first")}
@@ -126,57 +121,60 @@ def tile_picked_specacc_none_po_kernel(
         draft_part = {}
 
         def look_up_draft(t, slot):
-            draft_part[t] = keep.tile([P, V], F32, name=slot)
+            if t == first:
+                draft_part[t] = stage.tile([P, V], F32, name=slot, offset=3 * PLANE_BYTES)
+            else:
+                draft_part[t] = keep.tile([P, V], F32, name=slot)
             nc.vector.tensor_tensor(draft_part[t][:], e[t][:].indirect(accepted[:]), share[:], MULT)
 
-        y = {}
+        y, banks = {}, {}
 
         def target_plane(t, bank_no, slot):
             y[t] = keep.tile([P, S], F32, name=slot, align_bytes=64)
-            product(target_weights[t], y[t], bank_no, 0, S)
+            banks[t] = product(target_weights[t], y[t], bank_no, 0, S)
 
         product(draft_weights[second], e[second], 2, 0, S)
-        look_up_draft(first, "raw1_third")
+        look_up_draft(first, "draft_first")
         target_weights = quantise_weights(grouped1, "w1")
         look_up_draft(second, "draft_second")
         product(draft_weights[third], e[third], 3, 0, S)
         rest = keep.tile([P, V], F32, name="rest")
         nc.scalar.activation(rest[:], share[:], COPY, bias=1.0, scale=-1.0)
-        target_plane(first, 5, "y_first")
         product(draft_weights[last], e[last], 4, 0, S)
-        target_plane(second, 6, "y_second")
-        target_plane(third, 7, "y_third")
         look_up_draft(third, "draft_third")
         look_up_draft(last, "draft_last")
 
-        target_part = {}
+        target_part, out = {}, {}
 
         def look_up_target(t):
             target_part[t] = keep.tile([P, V], F32, name=f"target_part{t}", align_bytes=64)
             nc.vector.tensor_tensor(target_part[t][:], y[t][:].indirect(accepted[:]), rest[:], MULT)
 
+        def second_copy(t, slot):
+            out[t] = keep.tile([P, S], F32, name=slot, align_bytes=64)
+            nc.scalar.copy(out[t][:], banks[t][:])
+
         woven = keep.tile([P, S, PACK], BF16, name="woven", align_bytes=64)
         out_rows = out_0.rearrange("(p t) c -> p t c", t=PACK)
 
         def put_back(t):
-            nc.vector.tensor_tensor(y[t][:].indirect(accepted[:]), target_part[t][:], draft_part[t][:], ADD)
-            nc.sync.dma_start(out_rows[:, t, :], y[t][:])
+            nc.vector.tensor_tensor(out[t][:].indirect(accepted[:]), target_part[t][:], draft_part[t][:], ADD)
+            nc.sync.dma_start(out_rows[:, t, :], out[t][:])
 
-        look_up_target(first)
-        look_up_target(second)
-        put_back(first)
-        nc.scalar.copy(woven[:, :, first], y[first][:])
-        target_plane(last, 0, f"target_part{first}")
-        look_up_target(third)
-        put_back(second)
-        nc.scalar.copy(woven[:, :, second], y[second][:])
-        look_up_target(last)
-        put_back(third)
-        nc.scalar.copy(woven[:, :, third], y[third][:])
+        for i, t in enumerate(ORDER):
+            target_plane(t, TARGET_BANKS[i], f"y{t}")
+            look_up_target(t)
+            if i > 0:
+                second_copy(ORDER[i - 1], f"out{ORDER[i - 1]}")
+                put_back(ORDER[i - 1])
+        nc.scalar.copy(woven[:, :, first], out[first][:])
+        second_copy(last, f"target_part{first}")
+        nc.scalar.copy(woven[:, :, second], out[second][:])
+        nc.scalar.copy(woven[:, :, third], out[third][:])
         put_back(last)
-        nc.vector.tensor_copy(woven[:, :LAST_VECTOR_CUT, last], y[last][:, :LAST_VECTOR_CUT])
-        nc.vector.tensor_copy(woven[:, LAST_VECTOR_CUT:LAST_VECTOR, last], y[last][:, LAST_VECTOR_CUT:LAST_VECTOR])
-        nc.scalar.copy(woven[:, LAST_VECTOR:, last], y[last][:, LAST_VECTOR:])
+        nc.vector.tensor_copy(woven[:, :LAST_VECTOR_CUT, last], out[last][:, :LAST_VECTOR_CUT])
+        nc.vector.tensor_copy(woven[:, LAST_VECTOR_CUT:LAST_VECTOR, last], out[last][:, LAST_VECTOR_CUT:LAST_VECTOR])
+        nc.scalar.copy(woven[:, LAST_VECTOR:, last], out[last][:, LAST_VECTOR:])
 
         out_scales = keep.tile([P, S], U8, name="out_scales", align_bytes=64)
         out_words = out_1[0].rearrange("p c t -> p (c t)").bitcast(I32)

@@ -25,10 +25,10 @@ PLANE_BYTES = 4 * S
 ORDER = (0, 2, 3, 1)
 
 W2_VECTOR = 176
-W1_VECTOR = 344
+W1_VECTOR = 376
 FIRST_PLANE_PIECES = ((0, 0, 256), (1, 256, 384), (7, 384, 512))
 TARGET_BANKS = (5, 6, 7, 0)
-LAST_VECTOR_CUT, LAST_VECTOR = 128, 288
+LAST_VECTOR_CUT, LAST_VECTOR = 128, 320
 OUT_PIECES = ((0, 128), (128, 256), (256, 512))
 
 

@@ -66,6 +66,12 @@ def tile_picked_specacc_none_po_kernel(
                 raw[:, :, c0:c1].rearrange("p j (m t) -> p m j t", t=PACK),
             )
 
+        def round_pair(grouped, raw, t0, c0, c1, copy):
+            copy(
+                grouped[:, t0 : t0 + 2, c0 // PACK : c1 // PACK, :].rearrange("p t m j -> p m j t"),
+                raw[:, :, c0:c1].rearrange("p j (m t) -> p m j t", t=PACK)[:, :, :, t0 : t0 + 2],
+            )
+
         def quantise_weights(grouped, name):
             operands = {}
             for pair in range(2):
@@ -108,8 +114,9 @@ def tile_picked_specacc_none_po_kernel(
             nc.vector.tensor_copy(x_codes[:, h * half : (h + 1) * half], word_table[:].indirect(offsets))
 
         grouped1 = keep.tile([P, PACK, P, PACK], BF16, name="grouped1", align_bytes=64)
-        round_weights(grouped1, raw1, 0, 0, W1_VECTOR, nc.vector.tensor_copy)
-        round_weights(grouped1, raw1, 0, W1_VECTOR, N, nc.scalar.copy)
+        for t0 in (0, 2):
+            round_pair(grouped1, raw1, t0, 0, W1_VECTOR, nc.vector.tensor_copy)
+            round_pair(grouped1, raw1, t0, W1_VECTOR, N, nc.scalar.copy)
 
         first, second, third, last = ORDER
         e = {first: keep.tile([P, S], F32, name="e_first")}

@@ -28,8 +28,7 @@ W2_VECTOR = 176
 W1_VECTOR = 376
 FIRST_PLANE_PIECES = ((0, 0, 256), (1, 256, 384), (7, 384, 512))
 TARGET_BANKS = (5, 6, 7, 0)
-LAST_VECTOR_CUT, LAST_VECTOR = 128, 320
-OUT_PIECES = ((0, 128), (128, 256), (256, 512))
+OUT_PIECES = ((0, 128), (128, 256), (256, 384), (384, 512))
 
 
 def tile_picked_specacc_none_po_kernel(
@@ -179,9 +178,9 @@ def tile_picked_specacc_none_po_kernel(
         nc.scalar.copy(woven[:, :, second], out[second][:])
         nc.scalar.copy(woven[:, :, third], out[third][:])
         put_back(last)
-        nc.vector.tensor_copy(woven[:, :LAST_VECTOR_CUT, last], out[last][:, :LAST_VECTOR_CUT])
-        nc.vector.tensor_copy(woven[:, LAST_VECTOR_CUT:LAST_VECTOR, last], out[last][:, LAST_VECTOR_CUT:LAST_VECTOR])
-        nc.scalar.copy(woven[:, LAST_VECTOR:, last], out[last][:, LAST_VECTOR:])
+        for c0, c1 in OUT_PIECES:
+            copy = nc.vector.tensor_copy if c1 <= half else nc.scalar.copy
+            copy(woven[:, c0:c1, last], out[last][:, c0:c1])
 
         out_scales = keep.tile([P, S], U8, name="out_scales", align_bytes=64)
         out_words = out_1[0].rearrange("p c t -> p (c t)").bitcast(I32)
@@ -192,8 +191,9 @@ def tile_picked_specacc_none_po_kernel(
                 scales=out_scales[:, c0:c1],
                 in_=woven[:, c0:c1, :].rearrange("p c t -> p (c t)"),
             )
-            if c1 % half == 0:
-                nc.sync.dma_start(out_words[:, c1 - half : c1], out_codes[:, c1 - half : c1].bitcast(I32))
+            if c1 >= half:
+                stored = 0 if c1 == half else c0
+                nc.sync.dma_start(out_words[:, stored:c1], out_codes[:, stored:c1].bitcast(I32))
         for q in range(P // QUADRANT):
             queue = nc.scalar if q % 2 == 0 else nc.sync
             queue.dma_start(

@@ -25,7 +25,7 @@ PLANE_BYTES = 4 * S
 ORDER = (0, 2, 3, 1)
 
 W2_VECTOR = 176
-W1_VECTOR = 376
+W1_VECTOR = (376, 288)
 FIRST_PLANE_PIECES = ((0, 0, 256), (1, 256, 384), (7, 384, 512))
 TARGET_BANKS = (5, 6, 7, 0)
 OUT_PIECES = ((0, 128), (128, 256), (256, 384), (384, 512))
@@ -113,9 +113,9 @@ def tile_picked_specacc_none_po_kernel(
             nc.vector.tensor_copy(x_codes[:, h * half : (h + 1) * half], word_table[:].indirect(offsets))
 
         grouped1 = keep.tile([P, PACK, P, PACK], BF16, name="grouped1", align_bytes=64)
-        for t0 in (0, 2):
-            round_pair(grouped1, raw1, t0, 0, W1_VECTOR, nc.vector.tensor_copy)
-            round_pair(grouped1, raw1, t0, W1_VECTOR, N, nc.scalar.copy)
+        for t0, split in zip((0, 2), W1_VECTOR):
+            round_pair(grouped1, raw1, t0, 0, split, nc.vector.tensor_copy)
+            round_pair(grouped1, raw1, t0, split, N, nc.scalar.copy)
 
         first, second, third, last = ORDER
         e = {first: keep.tile([P, S], F32, name="e_first")}
@@ -191,9 +191,8 @@ def tile_picked_specacc_none_po_kernel(
                 scales=out_scales[:, c0:c1],
                 in_=woven[:, c0:c1, :].rearrange("p c t -> p (c t)"),
             )
-            if c1 >= half:
-                stored = 0 if c1 == half else c0
-                nc.sync.dma_start(out_words[:, stored:c1], out_codes[:, stored:c1].bitcast(I32))
+            if c1 % half == 0:
+                nc.sync.dma_start(out_words[:, c1 - half : c1], out_codes[:, c1 - half : c1].bitcast(I32))
         for q in range(P // QUADRANT):
             queue = nc.scalar if q % 2 == 0 else nc.sync
             queue.dma_start(

@@ -26,8 +26,6 @@ ORDER = (0, 2, 3, 1)
 
 W2_VECTOR = 176
 W1_VECTOR = (376, 288)
-FIRST_PLANE_PIECES = ((0, 0, 256), (1, 256, 384), (7, 384, 512))
-TARGET_BANKS = (5, 6, 7, 0)
 OUT_PIECES = ((0, 128), (128, 256), (256, 384), (384, 512))
 
 
@@ -52,132 +50,157 @@ def tile_picked_specacc_none_po_kernel(
             nc.sync.dma_start(scale_table[r:P:QUADRANT, :].bitcast(I32), x_scales[0, r:16:PACK, :].bitcast(I32))
         word_table = keep.tile([P, T], U32, name="word_table")
         nc.sync.dma_start(word_table[:].bitcast(I32), x_words[0].rearrange("p n t -> p (n t)").bitcast(I32))
-        raw1 = stage.tile([P, PACK, N], F32, name="raw1", offset=0)
+        raw1 = stage.tile([P, PACK, N], F32, name="raw1", offset=0, align_bytes=64)
         nc.sync.dma_start(raw1[:], w1.rearrange("(p j) c -> p j c", j=PACK))
         accepted = keep.tile([P, V // LIST_ROWS], U16, name="accepted")
         nc.sync.dma_start(accepted[:], acc_l)
         share = keep.tile([P, V], F32, name="share")
         nc.sync.dma_start(share[:], sh.rearrange("(p t) v -> p t v", t=PACK)[:, 0, :])
 
-        def round_weights(grouped, raw, base, c0, c1, copy):
+        def negate_on_vector(dest, src):
+            nc.vector.tensor_scalar_mul(dest, src, -1.0)
+
+        def negate_on_scalar(dest, src):
+            nc.scalar.activation(dest, src, COPY, scale=-1.0)
+
+        def round_weights(grouped, raw, c0, c1, copy):
             copy(
-                grouped[:, :, (base + c0) // PACK : (base + c1) // PACK, :].rearrange("p t m j -> p m j t"),
+                grouped[:, :, c0 // PACK : c1 // PACK, :].rearrange("p t m j -> p m j t"),
                 raw[:, :, c0:c1].rearrange("p j (m t) -> p m j t", t=PACK),
             )
 
         def round_pair(grouped, raw, t0, c0, c1, copy):
             copy(
-                grouped[:, t0 : t0 + 2, c0 // PACK : c1 // PACK, :].rearrange("p t m j -> p m j t"),
+                grouped[:, :, c0 // PACK : c1 // PACK, :].rearrange("p t m j -> p m j t"),
                 raw[:, :, c0:c1].rearrange("p j (m t) -> p m j t", t=PACK)[:, :, :, t0 : t0 + 2],
             )
 
-        def quantise_weights(grouped, name):
-            operands = {}
-            for pair in range(2):
-                codes = keep.tile([P, 2 * P], U32, name=f"codes_{name}{pair}", align_bytes=64)
-                scales = keep.tile([P, 2 * P], U8, name=f"scales_{name}{pair}", align_bytes=64)
-                nc.vector.quantize_mx(
-                    out=codes[:].bitcast(FP8X4),
-                    scales=scales[:],
-                    in_=grouped[:, 2 * pair : 2 * pair + 2, :, :].rearrange("p t m j -> p (t m j)"),
-                )
-                for i in range(2):
-                    operands[2 * pair + i] = (codes[:, i * P : (i + 1) * P], scales[:, i * P : (i + 1) * P])
-            return operands
+        def quantise_pair(grouped, name):
+            codes = keep.tile([P, 2 * P], U32, name=f"codes_{name}", align_bytes=64)
+            scales = keep.tile([P, 2 * P], U8, name=f"scales_{name}", align_bytes=64)
+            nc.vector.quantize_mx(
+                out=codes[:].bitcast(FP8X4), scales=scales[:], in_=grouped.rearrange("p t m j -> p (t m j)")
+            )
+            return [(codes[:, i * P : (i + 1) * P], scales[:, i * P : (i + 1) * P]) for i in range(2)]
 
-        def product(operand, dest, bank_no, c0, c1):
+        def mx_pass(bank, operand, c0, c1, start, stop):
             codes, scales = operand
-            bank = psum.tile([P, c1 - c0], F32, name=f"bank{bank_no}")
             nc.tensor.matmul_mx(
                 out=bank[:],
                 lhsT=codes.bitcast(FP8X4),
                 lhsT_scale=scales,
                 rhs=x_codes[:, c0:c1].bitcast(FP8X4),
                 rhs_scale=x_scale[:, c0:c1],
-                start=True,
-                stop=True,
+                start=start,
+                stop=stop,
             )
-            nc.scalar.copy(dest[:, c0:c1], bank[:])
-            return bank
+
+        def product(operand, dest, bank_no, c0, c1, copy):
+            bank = psum.tile([P, c1 - c0], F32, name=f"bank{bank_no}")
+            mx_pass(bank, operand, c0, c1, True, True)
+            copy(dest[:, c0:c1], bank[:])
+
+        def fetch(picked, plane):
+            nc.scalar.activation(picked[:], plane[:].indirect(accepted[:]), COPY)
+
+        def weigh(weighed, values, weights):
+            nc.vector.tensor_tensor(weighed[:], values, weights[:], MULT)
+
+        def small(name):
+            return keep.tile([P, V], F32, name=name, align_bytes=64)
 
         x_scale = keep.tile([P, S], U8, name="x_scale", align_bytes=64)
         nc.vector.tensor_copy(x_scale[:], scale_table[:].indirect(picks[:]))
         grouped2 = keep.tile([P, PACK, P, PACK], BF16, name="grouped2", align_bytes=64)
-        round_weights(grouped2, raw2, 0, 0, W2_VECTOR, nc.vector.tensor_copy)
-        round_weights(grouped2, raw2, 0, W2_VECTOR, N, nc.scalar.copy)
-        draft_weights = quantise_weights(grouped2, "w2")
+        round_weights(grouped2, raw2, 0, W2_VECTOR, negate_on_vector)
+        round_weights(grouped2, raw2, W2_VECTOR, N, negate_on_scalar)
+        draft_weights = quantise_pair(grouped2[:, 0:2], "w2a") + quantise_pair(grouped2[:, 2:4], "w2b")
         x_codes = keep.tile([P, S], U32, name="x_codes", align_bytes=64)
         half, half_list = S // 2, S // 2 // LIST_ROWS
         for h in range(2):
             offsets = picks[:, h * half_list : (h + 1) * half_list]
             nc.vector.tensor_copy(x_codes[:, h * half : (h + 1) * half], word_table[:].indirect(offsets))
 
-        grouped1 = keep.tile([P, PACK, P, PACK], BF16, name="grouped1", align_bytes=64)
-        for t0, split in zip((0, 2), W1_VECTOR):
-            round_pair(grouped1, raw1, t0, 0, split, nc.vector.tensor_copy)
-            round_pair(grouped1, raw1, t0, split, N, nc.scalar.copy)
-
         first, second, third, last = ORDER
-        e = {first: keep.tile([P, S], F32, name="e_first")}
-        for i, t in enumerate(ORDER[1:]):
-            e[t] = stage.tile([P, S], F32, name=f"e{t}", offset=PLANE_BYTES * i)
-        for bank_no, c0, c1 in FIRST_PLANE_PIECES:
-            product(draft_weights[first], e[first], bank_no, c0, c1)
+        e = {t: keep.tile([P, S], F32, name=f"e{t}") for t in (first, last)}
+        product(draft_weights[first], e[first], 0, 0, half, negate_on_scalar)
+        product(draft_weights[last], e[last], 1, 0, half, negate_on_scalar)
+        product(draft_weights[first], e[first], 2, half, S, negate_on_scalar)
+        product(draft_weights[last], e[last], 3, half, S, negate_on_vector)
+        gap_banks = {}
+        for t, bank_no in ((second, 4), (third, 5)):
+            gap_banks[t] = psum.tile([P, S], F32, name=f"bank{bank_no}")
+            mx_pass(gap_banks[t], draft_weights[t], 0, S, True, False)
 
-        draft_part = {}
+        raw1_bytes = PACK * PLANE_BYTES
+        grouped1 = []
+        for pair, split in enumerate(W1_VECTOR):
+            grouped1.append(
+                stage.tile([P, 2, P, PACK], BF16, name=f"grouped1_{pair}", offset=raw1_bytes + pair * PLANE_BYTES)
+            )
+            round_pair(grouped1[pair], raw1, 2 * pair, 0, split, nc.vector.tensor_copy)
+            round_pair(grouped1[pair], raw1, 2 * pair, split, N, nc.scalar.copy)
+        target_weights = quantise_pair(grouped1[0][:], "w1a") + quantise_pair(grouped1[1][:], "w1b")
 
-        def look_up_draft(t, slot):
-            if t == first:
-                draft_part[t] = stage.tile([P, V], F32, name=slot, offset=3 * PLANE_BYTES)
-            else:
-                draft_part[t] = keep.tile([P, V], F32, name=slot)
-            nc.vector.tensor_tensor(draft_part[t][:], e[t][:].indirect(accepted[:]), share[:], MULT)
+        rest = small("rest")
+        nc.scalar.activation(rest[:], share[:], COPY, bias=1.0, scale=-1.0)
+        fetched_e = stage.tile([P, V], F32, name="fetched_e", offset=0)
+        fetch(fetched_e, e[first])
+        draft_part = {
+            last: stage.tile([P, V], F32, name="draft_last", offset=raw1_bytes),
+            first: small("draft_first"),
+        }
+        weigh(draft_part[last], e[last][:].indirect(accepted[:]), share)
+        weigh(draft_part[first], fetched_e[:], share)
 
-        y, banks = {}, {}
+        out, gap, target_part = {}, {}, {}
+        out_rows = out_0.rearrange("(p t) c -> p t c", t=PACK)
 
         def target_plane(t, bank_no, slot):
-            y[t] = keep.tile([P, S], F32, name=slot, align_bytes=64)
-            banks[t] = product(target_weights[t], y[t], bank_no, 0, S)
-
-        product(draft_weights[second], e[second], 2, 0, S)
-        look_up_draft(first, "draft_first")
-        target_weights = quantise_weights(grouped1, "w1")
-        look_up_draft(second, "draft_second")
-        product(draft_weights[third], e[third], 3, 0, S)
-        rest = keep.tile([P, V], F32, name="rest")
-        nc.scalar.activation(rest[:], share[:], COPY, bias=1.0, scale=-1.0)
-        product(draft_weights[last], e[last], 4, 0, S)
-        look_up_draft(third, "draft_third")
-        look_up_draft(last, "draft_last")
-
-        target_part, out = {}, {}
-
-        def look_up_target(t):
-            target_part[t] = keep.tile([P, V], F32, name=f"target_part{t}", align_bytes=64)
-            nc.vector.tensor_tensor(target_part[t][:], y[t][:].indirect(accepted[:]), rest[:], MULT)
-
-        def second_copy(t, slot):
             out[t] = keep.tile([P, S], F32, name=slot, align_bytes=64)
-            nc.scalar.copy(out[t][:], banks[t][:])
+            product(target_weights[t], out[t], bank_no, 0, S, nc.scalar.copy)
 
-        woven = keep.tile([P, S, PACK], BF16, name="woven", align_bytes=64)
-        out_rows = out_0.rearrange("(p t) c -> p t c", t=PACK)
+        def gap_plane(t):
+            gap[t] = keep.tile([P, S], F32, name=f"gap{t}")
+            mx_pass(gap_banks[t], target_weights[t], 0, S, False, True)
+            negate_on_scalar(gap[t][:], gap_banks[t][:])
+
+        def weigh_target(t):
+            target_part[t] = small(f"target{t}")
+            weigh(target_part[t], out[t][:].indirect(accepted[:]), rest)
+
+        def weigh_gap(t):
+            draft_part[t] = small(f"draft{t}")
+            weigh(draft_part[t], gap[t][:].indirect(accepted[:]), share)
+
+        def fetch_target(t):
+            target_part[t] = small(f"target{t}")
+            fetch(target_part[t], out[t])
 
         def put_back(t):
             nc.vector.tensor_tensor(out[t][:].indirect(accepted[:]), target_part[t][:], draft_part[t][:], ADD)
             nc.sync.dma_start(out_rows[:, t, :], out[t][:])
 
-        for i, t in enumerate(ORDER):
-            target_plane(t, TARGET_BANKS[i], f"y{t}")
-            look_up_target(t)
-            if i > 0:
-                second_copy(ORDER[i - 1], f"out{ORDER[i - 1]}")
-                put_back(ORDER[i - 1])
+        woven = keep.tile([P, S, PACK], BF16, name="woven", align_bytes=64)
+        target_plane(first, 6, "out_first")
+        weigh_target(first)
+        put_back(first)
+        gap_plane(second)
+        weigh_gap(second)
+        target_plane(second, 7, "out_second")
+        gap_plane(third)
+        weigh_gap(third)
+        fetch_target(second)
+        put_back(second)
+        target_plane(third, 0, "out_third")
         nc.scalar.copy(woven[:, :, first], out[first][:])
-        second_copy(last, f"target_part{first}")
-        nc.scalar.copy(woven[:, :, second], out[second][:])
-        nc.scalar.copy(woven[:, :, third], out[third][:])
+        target_plane(last, 1, f"target{first}")
+        weigh_target(last)
+        fetch_target(third)
+        put_back(third)
         put_back(last)
+        for t in (second, third):
+            nc.scalar.copy(woven[:, :, t], out[t][:])
         for c0, c1 in OUT_PIECES:
             copy = nc.vector.tensor_copy if c1 <= half else nc.scalar.copy
             copy(woven[:, c0:c1, last], out[last][:, c0:c1])

@@ -142,8 +142,8 @@ def tile_picked_specacc_none_po_kernel(
             round_pair(grouped1[pair], raw1, 2 * pair, split, N, nc.scalar.copy)
         target_weights = quantise_pair(grouped1[0][:], "w1a") + quantise_pair(grouped1[1][:], "w1b")
 
-        rest = small("rest")
-        nc.scalar.activation(rest[:], share[:], COPY, bias=1.0, scale=-1.0)
+        rest = stage.tile([P, V], F32, name="rest", offset=raw1_bytes + PLANE_BYTES // 2)
+        nc.vector.tensor_scalar(rest[:], share[:], -1.0, 1.0, MULT, ADD)
         fetched_e = stage.tile([P, V], F32, name="fetched_e", offset=0)
         fetch(fetched_e, e[first])
         draft_part = {

@@ -144,14 +144,12 @@ def tile_picked_specacc_none_po_kernel(
 
         rest = stage.tile([P, V], F32, name="rest", offset=raw1_bytes + PLANE_BYTES // 2)
         nc.vector.tensor_scalar(rest[:], share[:], -1.0, 1.0, MULT, ADD)
-        fetched_e = stage.tile([P, V], F32, name="fetched_e", offset=0)
-        fetch(fetched_e, e[first])
         draft_part = {
             last: stage.tile([P, V], F32, name="draft_last", offset=raw1_bytes),
-            first: small("draft_first"),
+            first: stage.tile([P, V], F32, name="draft_first", offset=raw1_bytes + PLANE_BYTES),
         }
         weigh(draft_part[last], e[last][:].indirect(accepted[:]), share)
-        weigh(draft_part[first], fetched_e[:], share)
+        weigh(draft_part[first], e[first][:].indirect(accepted[:]), share)
 
         out, gap, target_part = {}, {}, {}
         out_rows = out_0.rearrange("(p t) c -> p t c", t=PACK)

@@ -24,8 +24,9 @@ PLANE_BYTES = 4 * S
 
 ORDER = (0, 2, 3, 1)
 
-W2_VECTOR = 176
+W2_VECTOR = 336
 W1_VECTOR = (376, 288)
+FIRST_PLANE_PIECES = ((0, 0, 256), (1, 256, 384), (2, 384, 512))
 OUT_PIECES = ((0, 128), (128, 256), (256, 384), (384, 512))
 
 
@@ -48,7 +49,7 @@ def tile_picked_specacc_none_po_kernel(
         nc.sync.dma_start(picks[:], offs)
         for r in range(PACK):
             nc.sync.dma_start(scale_table[r:P:QUADRANT, :].bitcast(I32), x_scales[0, r:16:PACK, :].bitcast(I32))
-        word_table = keep.tile([P, T], U32, name="word_table")
+        word_table = keep.tile([P, T], U32, name="word_table", align_bytes=64)
         nc.sync.dma_start(word_table[:].bitcast(I32), x_words[0].rearrange("p n t -> p (n t)").bitcast(I32))
         raw1 = stage.tile([P, PACK, N], F32, name="raw1", offset=0, align_bytes=64)
         nc.sync.dma_start(raw1[:], w1.rearrange("(p j) c -> p j c", j=PACK))
@@ -57,17 +58,8 @@ def tile_picked_specacc_none_po_kernel(
         share = keep.tile([P, V], F32, name="share")
         nc.sync.dma_start(share[:], sh.rearrange("(p t) v -> p t v", t=PACK)[:, 0, :])
 
-        def negate_on_vector(dest, src):
-            nc.vector.tensor_scalar_mul(dest, src, -1.0)
-
         def negate_on_scalar(dest, src):
             nc.scalar.activation(dest, src, COPY, scale=-1.0)
-
-        def round_weights(grouped, raw, c0, c1, copy):
-            copy(
-                grouped[:, :, c0 // PACK : c1 // PACK, :].rearrange("p t m j -> p m j t"),
-                raw[:, :, c0:c1].rearrange("p j (m t) -> p m j t", t=PACK),
-            )
 
         def round_pair(grouped, raw, t0, c0, c1, copy):
             copy(
@@ -75,8 +67,8 @@ def tile_picked_specacc_none_po_kernel(
                 raw[:, :, c0:c1].rearrange("p j (m t) -> p m j t", t=PACK)[:, :, :, t0 : t0 + 2],
             )
 
-        def quantise_pair(grouped, name):
-            codes = keep.tile([P, 2 * P], U32, name=f"codes_{name}", align_bytes=64)
+        def quantise_pair(grouped, name, slot=None):
+            codes = keep.tile([P, 2 * P], U32, name=slot or f"codes_{name}", align_bytes=64)
             scales = keep.tile([P, 2 * P], U8, name=f"scales_{name}", align_bytes=64)
             nc.vector.quantize_mx(
                 out=codes[:].bitcast(FP8X4), scales=scales[:], in_=grouped.rearrange("p t m j -> p (t m j)")
@@ -111,22 +103,23 @@ def tile_picked_specacc_none_po_kernel(
 
         x_scale = keep.tile([P, S], U8, name="x_scale", align_bytes=64)
         nc.vector.tensor_copy(x_scale[:], scale_table[:].indirect(picks[:]))
-        grouped2 = keep.tile([P, PACK, P, PACK], BF16, name="grouped2", align_bytes=64)
-        round_weights(grouped2, raw2, 0, W2_VECTOR, negate_on_vector)
-        round_weights(grouped2, raw2, W2_VECTOR, N, negate_on_scalar)
-        draft_weights = quantise_pair(grouped2[:, 0:2], "w2a") + quantise_pair(grouped2[:, 2:4], "w2b")
+        grouped2 = [keep.tile([P, 2, P, PACK], BF16, name=f"grouped2_{pair}", align_bytes=64) for pair in range(2)]
+        round_pair(grouped2[0], raw2, 0, 0, W2_VECTOR, nc.vector.tensor_copy)
+        round_pair(grouped2[0], raw2, 0, W2_VECTOR, N, nc.scalar.copy)
+        round_pair(grouped2[1], raw2, 2, 0, N, negate_on_scalar)
+        draft_weights = quantise_pair(grouped2[0][:], "w2a")
         x_codes = keep.tile([P, S], U32, name="x_codes", align_bytes=64)
         half, half_list = S // 2, S // 2 // LIST_ROWS
         for h in range(2):
             offsets = picks[:, h * half_list : (h + 1) * half_list]
             nc.vector.tensor_copy(x_codes[:, h * half : (h + 1) * half], word_table[:].indirect(offsets))
 
+        draft_weights = draft_weights + quantise_pair(grouped2[1][:], "w2b", "word_table")
+
         first, second, third, last = ORDER
-        e = {t: keep.tile([P, S], F32, name=f"e{t}") for t in (first, last)}
-        product(draft_weights[first], e[first], 0, 0, half, negate_on_scalar)
-        product(draft_weights[last], e[last], 1, 0, half, negate_on_scalar)
-        product(draft_weights[first], e[first], 2, half, S, negate_on_scalar)
-        product(draft_weights[last], e[last], 3, half, S, negate_on_vector)
+        e = {first: keep.tile([P, S], F32, name="e_first"), last: stage.tile([P, S], F32, name="e_last", offset=0)}
+        for bank_no, c0, c1 in FIRST_PLANE_PIECES:
+            product(draft_weights[first], e[first], bank_no, c0, c1, nc.scalar.copy)
         gap_banks = {}
         for t, bank_no in ((second, 4), (third, 5)):
             gap_banks[t] = psum.tile([P, S], F32, name=f"bank{bank_no}")
@@ -142,14 +135,15 @@ def tile_picked_specacc_none_po_kernel(
             round_pair(grouped1[pair], raw1, 2 * pair, split, N, nc.scalar.copy)
         target_weights = quantise_pair(grouped1[0][:], "w1a") + quantise_pair(grouped1[1][:], "w1b")
 
+        product(draft_weights[last], e[last], 3, 0, S, nc.scalar.copy)
         rest = stage.tile([P, V], F32, name="rest", offset=raw1_bytes + PLANE_BYTES // 2)
         nc.vector.tensor_scalar(rest[:], share[:], -1.0, 1.0, MULT, ADD)
         draft_part = {
-            last: stage.tile([P, V], F32, name="draft_last", offset=raw1_bytes),
-            first: stage.tile([P, V], F32, name="draft_first", offset=raw1_bytes + PLANE_BYTES),
+            last: small("draft_last"),
+            first: stage.tile([P, V], F32, name="draft_first", offset=raw1_bytes),
         }
-        weigh(draft_part[last], e[last][:].indirect(accepted[:]), share)
         weigh(draft_part[first], e[first][:].indirect(accepted[:]), share)
+        weigh(draft_part[last], e[last][:].indirect(accepted[:]), share)
 
         out, gap, target_part = {}, {}, {}
         out_rows = out_0.rearrange("(p t) c -> p t c", t=PACK)

@@ -25,7 +25,7 @@ PLANE_BYTES = 4 * S
 ORDER = (0, 2, 3, 1)
 
 W2_VECTOR = 336
-W1_VECTOR = (376, 288)
+W1_VECTOR = (512, 288)
 FIRST_PLANE_PIECES = ((0, 0, 256), (1, 256, 384), (2, 384, 512))
 OUT_PIECES = ((0, 128), (128, 256), (256, 384), (384, 512))
 
@@ -132,7 +132,8 @@ def tile_picked_specacc_none_po_kernel(
                 stage.tile([P, 2, P, PACK], BF16, name=f"grouped1_{pair}", offset=raw1_bytes + pair * PLANE_BYTES)
             )
             round_pair(grouped1[pair], raw1, 2 * pair, 0, split, nc.vector.tensor_copy)
-            round_pair(grouped1[pair], raw1, 2 * pair, split, N, nc.scalar.copy)
+            if split < N:
+                round_pair(grouped1[pair], raw1, 2 * pair, split, N, nc.scalar.copy)
         target_weights = quantise_pair(grouped1[0][:], "w1a") + quantise_pair(grouped1[1][:], "w1b")
 
         product(draft_weights[last], e[last], 3, 0, S, nc.scalar.copy)

@@ -27,6 +27,7 @@ ORDER = (0, 2, 3, 1)
 W2_VECTOR = 336
 W1_VECTOR = (512, 288)
 FIRST_PLANE_PIECES = ((0, 0, 256), (1, 256, 384), (2, 384, 512))
+FIRST_VECTOR = 128
 OUT_PIECES = ((0, 128), (128, 256), (256, 384), (384, 512))
 
 
@@ -136,6 +137,8 @@ def tile_picked_specacc_none_po_kernel(
                 round_pair(grouped1[pair], raw1, 2 * pair, split, N, nc.scalar.copy)
         target_weights = quantise_pair(grouped1[0][:], "w1a") + quantise_pair(grouped1[1][:], "w1b")
 
+        fetched_e = small("fetched_e")
+        fetch(fetched_e, e[first])
         product(draft_weights[last], e[last], 3, 0, S, nc.scalar.copy)
         rest = stage.tile([P, V], F32, name="rest", offset=raw1_bytes + PLANE_BYTES // 2)
         nc.vector.tensor_scalar(rest[:], share[:], -1.0, 1.0, MULT, ADD)
@@ -143,7 +146,7 @@ def tile_picked_specacc_none_po_kernel(
             last: small("draft_last"),
             first: stage.tile([P, V], F32, name="draft_first", offset=raw1_bytes),
         }
-        weigh(draft_part[first], e[first][:].indirect(accepted[:]), share)
+        weigh(draft_part[first], fetched_e[:], share)
         weigh(draft_part[last], e[last][:].indirect(accepted[:]), share)
 
         out, gap, target_part = {}, {}, {}
@@ -180,13 +183,14 @@ def tile_picked_specacc_none_po_kernel(
         put_back(first)
         gap_plane(second)
         weigh_gap(second)
+        nc.vector.tensor_copy(woven[:, :FIRST_VECTOR, first], out[first][:, :FIRST_VECTOR])
         target_plane(second, 7, "out_second")
         gap_plane(third)
         weigh_gap(third)
         fetch_target(second)
         put_back(second)
         target_plane(third, 0, "out_third")
-        nc.scalar.copy(woven[:, :, first], out[first][:])
+        nc.scalar.copy(woven[:, FIRST_VECTOR:, first], out[first][:, FIRST_VECTOR:])
         target_plane(last, 1, f"target{first}")
         weigh_target(last)
         fetch_target(third)

@@ -27,7 +27,7 @@ ORDER = (0, 2, 3, 1)
 W2_VECTOR = 336
 W1_VECTOR = (512, 288)
 FIRST_PLANE_PIECES = ((0, 0, 256), (1, 256, 384), (2, 384, 512))
-FIRST_VECTOR = 128
+MIDDLE_SCALAR = 288
 OUT_PIECES = ((0, 128), (128, 256), (256, 384), (384, 512))
 
 
@@ -61,6 +61,9 @@ def tile_picked_specacc_none_po_kernel(
 
         def negate_on_scalar(dest, src):
             nc.scalar.activation(dest, src, COPY, scale=-1.0)
+
+        def negate_on_vector(dest, src):
+            nc.vector.tensor_scalar(dest, src, -1.0, None, MULT)
 
         def round_pair(grouped, raw, t0, c0, c1, copy):
             copy(
@@ -105,8 +108,8 @@ def tile_picked_specacc_none_po_kernel(
         x_scale = keep.tile([P, S], U8, name="x_scale", align_bytes=64)
         nc.vector.tensor_copy(x_scale[:], scale_table[:].indirect(picks[:]))
         grouped2 = [keep.tile([P, 2, P, PACK], BF16, name=f"grouped2_{pair}", align_bytes=64) for pair in range(2)]
-        round_pair(grouped2[0], raw2, 0, 0, W2_VECTOR, nc.vector.tensor_copy)
-        round_pair(grouped2[0], raw2, 0, W2_VECTOR, N, nc.scalar.copy)
+        round_pair(grouped2[0], raw2, 0, 0, W2_VECTOR, negate_on_vector)
+        round_pair(grouped2[0], raw2, 0, W2_VECTOR, N, negate_on_scalar)
         round_pair(grouped2[1], raw2, 2, 0, N, negate_on_scalar)
         draft_weights = quantise_pair(grouped2[0][:], "w2a")
         x_codes = keep.tile([P, S], U32, name="x_codes", align_bytes=64)
@@ -118,11 +121,11 @@ def tile_picked_specacc_none_po_kernel(
         draft_weights = draft_weights + quantise_pair(grouped2[1][:], "w2b", "word_table")
 
         first, second, third, last = ORDER
-        e = {first: keep.tile([P, S], F32, name="e_first"), last: stage.tile([P, S], F32, name="e_last", offset=0)}
+        e = {first: keep.tile([P, S], F32, name="e_first"), third: stage.tile([P, S], F32, name="e_third", offset=0)}
         for bank_no, c0, c1 in FIRST_PLANE_PIECES:
-            product(draft_weights[first], e[first], bank_no, c0, c1, nc.scalar.copy)
+            product(draft_weights[first], e[first], bank_no, c0, c1, negate_on_scalar)
         gap_banks = {}
-        for t, bank_no in ((second, 4), (third, 5)):
+        for t, bank_no in ((second, 4), (last, 5)):
             gap_banks[t] = psum.tile([P, S], F32, name=f"bank{bank_no}")
             mx_pass(gap_banks[t], draft_weights[t], 0, S, True, False)
 
@@ -139,68 +142,88 @@ def tile_picked_specacc_none_po_kernel(
 
         fetched_e = small("fetched_e")
         fetch(fetched_e, e[first])
-        product(draft_weights[last], e[last], 3, 0, S, nc.scalar.copy)
+        product(draft_weights[third], e[third], 3, 0, S, negate_on_scalar)
         rest = stage.tile([P, V], F32, name="rest", offset=raw1_bytes + PLANE_BYTES // 2)
         nc.vector.tensor_scalar(rest[:], share[:], -1.0, 1.0, MULT, ADD)
         draft_part = {
-            last: small("draft_last"),
+            third: small("draft_third"),
             first: stage.tile([P, V], F32, name="draft_first", offset=raw1_bytes),
         }
         weigh(draft_part[first], fetched_e[:], share)
-        weigh(draft_part[last], e[last][:].indirect(accepted[:]), share)
+        weigh(draft_part[third], e[third][:].indirect(accepted[:]), share)
 
-        out, gap, target_part = {}, {}, {}
+        out, gap, target_part, fetched, mixed = {}, {}, {}, {}, {}
         out_rows = out_0.rearrange("(p t) c -> p t c", t=PACK)
 
-        def target_plane(t, bank_no, slot):
-            out[t] = keep.tile([P, S], F32, name=slot, align_bytes=64)
+        def target_plane(t, bank_no):
+            out[t] = keep.tile([P, S], F32, name=f"out{t}", align_bytes=64)
             product(target_weights[t], out[t], bank_no, 0, S, nc.scalar.copy)
 
-        def gap_plane(t):
-            gap[t] = keep.tile([P, S], F32, name=f"gap{t}")
+        def gap_plane(t, slot):
+            gap[t] = keep.tile([P, S], F32, name=slot, align_bytes=64)
             mx_pass(gap_banks[t], target_weights[t], 0, S, False, True)
             negate_on_scalar(gap[t][:], gap_banks[t][:])
-
-        def weigh_target(t):
-            target_part[t] = small(f"target{t}")
-            weigh(target_part[t], out[t][:].indirect(accepted[:]), rest)
-
-        def weigh_gap(t):
-            draft_part[t] = small(f"draft{t}")
-            weigh(draft_part[t], gap[t][:].indirect(accepted[:]), share)
+            fetched[t] = small(f"fetched{t}")
 
         def fetch_target(t):
             target_part[t] = small(f"target{t}")
             fetch(target_part[t], out[t])
 
+        def mix_on_gpsimd(t, values, weights, other, weighed):
+            mixed[t] = small(f"mixed{t}")
+            nc.gpsimd.tensor_tensor(weighed[:], values[:], weights[:], MULT)
+            nc.gpsimd.tensor_tensor(mixed[t][:], weighed[:], other[:], ADD)
+
         def put_back(t):
-            nc.vector.tensor_tensor(out[t][:].indirect(accepted[:]), target_part[t][:], draft_part[t][:], ADD)
+            nc.vector.tensor_copy(out[t][:].indirect(accepted[:]), mixed[t][:])
             nc.sync.dma_start(out_rows[:, t, :], out[t][:])
 
-        woven = keep.tile([P, S, PACK], BF16, name="woven", align_bytes=64)
-        target_plane(first, 6, "out_first")
-        weigh_target(first)
-        put_back(first)
-        gap_plane(second)
-        weigh_gap(second)
-        nc.vector.tensor_copy(woven[:, :FIRST_VECTOR, first], out[first][:, :FIRST_VECTOR])
-        target_plane(second, 7, "out_second")
-        gap_plane(third)
-        weigh_gap(third)
+        def round_on_gpsimd(dest, src):
+            nc.gpsimd.tensor_scalar(dest, src, 1.0, 0.0, MULT, ADD)
+
+        def weave(t, c0, c1, copy):
+            h = c0 // half
+            copy(woven[h][:, c0 - h * half : c1 - h * half, t], out[t][:, c0:c1])
+
+        out[first] = keep.tile([P, S], F32, name="out_first", align_bytes=64)
+        product(target_weights[first], out[first], 6, 0, half, nc.scalar.copy)
+        product(target_weights[first], out[first], 1, half, S, nc.scalar.copy)
+        target_part[first] = small("target_first")
+        weigh(target_part[first], out[first][:].indirect(accepted[:]), rest)
+        nc.vector.tensor_tensor(out[first][:].indirect(accepted[:]), target_part[first][:], draft_part[first][:], ADD)
+        nc.sync.dma_start(out_rows[:, first, :], out[first][:])
+        target_plane(second, 7)
+        gap_plane(second, "gap_second")
         fetch_target(second)
+        fetch(fetched[second], gap[second])
+        woven = [keep.tile([P, half, PACK], BF16, name="gap_second", align_bytes=64)]
+        draft_part[second] = small("weighed")
+        mixed[second] = small("mixed_second")
+        weigh(draft_part[second], fetched[second][:], share)
+        weave(first, 0, P, nc.vector.tensor_copy)
+        nc.vector.tensor_tensor(mixed[second][:], target_part[second][:], draft_part[second][:], ADD)
+        weave(first, P, half, nc.vector.tensor_copy)
         put_back(second)
-        target_plane(third, 0, "out_third")
-        nc.scalar.copy(woven[:, FIRST_VECTOR:, first], out[first][:, FIRST_VECTOR:])
-        target_plane(last, 1, f"target{first}")
-        weigh_target(last)
+        target_plane(third, 0)
         fetch_target(third)
+        mix_on_gpsimd(third, target_part[third], rest, draft_part[third], small("weighed"))
         put_back(third)
+        gap_plane(last, f"target{second}")
+        target_plane(last, 0)
+        fetch(fetched[last], gap[last])
+        fetch_target(last)
+        mix_on_gpsimd(last, fetched[last], share, target_part[last], small("woven_right"))
         put_back(last)
+        woven.append(keep.tile([P, half, PACK], BF16, name="woven_right", align_bytes=64))
+        weave(second, 0, half, nc.scalar.copy)
+        weave(first, half, S, nc.scalar.copy)
+        weave(third, 0, half, nc.scalar.copy)
         for t in (second, third):
-            nc.scalar.copy(woven[:, :, t], out[t][:])
+            weave(t, MIDDLE_SCALAR, S, round_on_gpsimd)
+        for t in (second, third):
+            weave(t, half, MIDDLE_SCALAR, nc.scalar.copy)
         for c0, c1 in OUT_PIECES:
-            copy = nc.vector.tensor_copy if c1 <= half else nc.scalar.copy
-            copy(woven[:, c0:c1, last], out[last][:, c0:c1])
+            weave(last, c0, c1, nc.vector.tensor_copy if c1 <= half else nc.scalar.copy)
 
         out_scales = keep.tile([P, S], U8, name="out_scales", align_bytes=64)
         out_words = out_1[0].rearrange("p c t -> p (c t)").bitcast(I32)
@@ -209,7 +232,7 @@ def tile_picked_specacc_none_po_kernel(
             nc.vector.quantize_mx(
                 out=out_codes[:, c0:c1].bitcast(FP8X4),
                 scales=out_scales[:, c0:c1],
-                in_=woven[:, c0:c1, :].rearrange("p c t -> p (c t)"),
+                in_=woven[c0 // half][:, c0 % half : c0 % half + c1 - c0, :].rearrange("p c t -> p (c t)"),
             )
             if c1 % half == 0:
                 nc.sync.dma_start(out_words[:, c1 - half : c1], out_codes[:, c1 - half : c1].bitcast(I32))

@@ -27,7 +27,7 @@ ORDER = (0, 2, 3, 1)
 W2_VECTOR = 336
 W1_VECTOR = (512, 288)
 FIRST_PLANE_PIECES = ((0, 0, 256), (1, 256, 384), (2, 384, 512))
-MIDDLE_SCALAR = 288
+FIRST_VECTOR = 128
 OUT_PIECES = ((0, 128), (128, 256), (256, 384), (384, 512))
 
 
@@ -39,6 +39,7 @@ def tile_picked_specacc_none_po_kernel(
         keep = ctx.enter_context(tc.tile_pool(name="keep", bufs=1))
         psum = ctx.enter_context(tc.psum_pool(name="psum", bufs=1))
         stage = ctx.enter_context(tc.tile_pool(name="stage", bufs=1))
+        late = ctx.enter_context(tc.tile_pool(name="late", bufs=1))
 
         scale_table = keep.tile([P, T], U8, name="scale_table")
         nc.vector.memset(scale_table[:, : T // 2].bitcast(I32), 0)
@@ -82,7 +83,7 @@ def tile_picked_specacc_none_po_kernel(
         def mx_pass(bank, operand, c0, c1, start, stop):
             codes, scales = operand
             nc.tensor.matmul_mx(
-                out=bank[:],
+                out=bank,
                 lhsT=codes.bitcast(FP8X4),
                 lhsT_scale=scales,
                 rhs=x_codes[:, c0:c1].bitcast(FP8X4),
@@ -93,7 +94,7 @@ def tile_picked_specacc_none_po_kernel(
 
         def product(operand, dest, bank_no, c0, c1, copy):
             bank = psum.tile([P, c1 - c0], F32, name=f"bank{bank_no}")
-            mx_pass(bank, operand, c0, c1, True, True)
+            mx_pass(bank[:], operand, c0, c1, True, True)
             copy(dest[:, c0:c1], bank[:])
 
         def fetch(picked, plane):
@@ -121,13 +122,15 @@ def tile_picked_specacc_none_po_kernel(
         draft_weights = draft_weights + quantise_pair(grouped2[1][:], "w2b", "word_table")
 
         first, second, third, last = ORDER
-        e = {first: keep.tile([P, S], F32, name="e_first"), third: stage.tile([P, S], F32, name="e_third", offset=0)}
+        e = {first: keep.tile([P, S], F32, name="e_first"), second: stage.tile([P, S], F32, name="e_second", offset=0)}
+        gap_banks = {t: psum.tile([P, S], F32, name=f"bank{bank_no}") for t, bank_no in ((third, 4), (last, 5))}
         for bank_no, c0, c1 in FIRST_PLANE_PIECES:
             product(draft_weights[first], e[first], bank_no, c0, c1, negate_on_scalar)
-        gap_banks = {}
-        for t, bank_no in ((second, 4), (last, 5)):
-            gap_banks[t] = psum.tile([P, S], F32, name=f"bank{bank_no}")
-            mx_pass(gap_banks[t], draft_weights[t], 0, S, True, False)
+            if c1 % half == 0:
+                mx_pass(gap_banks[last][:, c1 - half : c1], draft_weights[last], c1 - half, c1, c1 == half, False)
+        second_bank = psum.tile([P, S], F32, name="bank3")
+        mx_pass(second_bank[:], draft_weights[second], 0, S, True, True)
+        mx_pass(gap_banks[third][:], draft_weights[third], 0, S, True, False)
 
         raw1_bytes = PACK * PLANE_BYTES
         grouped1 = []
@@ -142,15 +145,15 @@ def tile_picked_specacc_none_po_kernel(
 
         fetched_e = small("fetched_e")
         fetch(fetched_e, e[first])
-        product(draft_weights[third], e[third], 3, 0, S, negate_on_scalar)
+        negate_on_scalar(e[second][:], second_bank[:])
         rest = stage.tile([P, V], F32, name="rest", offset=raw1_bytes + PLANE_BYTES // 2)
         nc.vector.tensor_scalar(rest[:], share[:], -1.0, 1.0, MULT, ADD)
         draft_part = {
-            third: small("draft_third"),
+            second: small("draft_second"),
             first: stage.tile([P, V], F32, name="draft_first", offset=raw1_bytes),
         }
         weigh(draft_part[first], fetched_e[:], share)
-        weigh(draft_part[third], e[third][:].indirect(accepted[:]), share)
+        weigh(draft_part[second], e[second][:].indirect(accepted[:]), share)
 
         out, gap, target_part, fetched, mixed = {}, {}, {}, {}, {}
         out_rows = out_0.rearrange("(p t) c -> p t c", t=PACK)
@@ -159,20 +162,15 @@ def tile_picked_specacc_none_po_kernel(
             out[t] = keep.tile([P, S], F32, name=f"out{t}", align_bytes=64)
             product(target_weights[t], out[t], bank_no, 0, S, nc.scalar.copy)
 
-        def gap_plane(t, slot):
-            gap[t] = keep.tile([P, S], F32, name=slot, align_bytes=64)
-            mx_pass(gap_banks[t], target_weights[t], 0, S, False, True)
+        def gap_plane(t, tile):
+            gap[t] = tile
+            mx_pass(gap_banks[t][:], target_weights[t], 0, S, False, True)
             negate_on_scalar(gap[t][:], gap_banks[t][:])
             fetched[t] = small(f"fetched{t}")
 
         def fetch_target(t):
             target_part[t] = small(f"target{t}")
             fetch(target_part[t], out[t])
-
-        def mix_on_gpsimd(t, values, weights, other, weighed):
-            mixed[t] = small(f"mixed{t}")
-            nc.gpsimd.tensor_tensor(weighed[:], values[:], weights[:], MULT)
-            nc.gpsimd.tensor_tensor(mixed[t][:], weighed[:], other[:], ADD)
 
         def put_back(t):
             nc.vector.tensor_copy(out[t][:].indirect(accepted[:]), mixed[t][:])
@@ -192,36 +190,42 @@ def tile_picked_specacc_none_po_kernel(
         weigh(target_part[first], out[first][:].indirect(accepted[:]), rest)
         nc.vector.tensor_tensor(out[first][:].indirect(accepted[:]), target_part[first][:], draft_part[first][:], ADD)
         nc.sync.dma_start(out_rows[:, first, :], out[first][:])
+
         target_plane(second, 7)
-        gap_plane(second, "gap_second")
+        gap_plane(third, late.tile([P, S], F32, name="gap_third", offset=PLANE_BYTES // 2, align_bytes=64))
         fetch_target(second)
-        fetch(fetched[second], gap[second])
-        woven = [keep.tile([P, half, PACK], BF16, name="gap_second", align_bytes=64)]
-        draft_part[second] = small("weighed")
-        mixed[second] = small("mixed_second")
-        weigh(draft_part[second], fetched[second][:], share)
-        weave(first, 0, P, nc.vector.tensor_copy)
-        nc.vector.tensor_tensor(mixed[second][:], target_part[second][:], draft_part[second][:], ADD)
-        weave(first, P, half, nc.vector.tensor_copy)
+        fetch(fetched[third], gap[third])
+        woven = [late.tile([P, half, PACK], BF16, name="woven_left", offset=0, align_bytes=64)]
+        mixed[second] = late.tile([P, V], F32, name="mixed_second", offset=PLANE_BYTES, align_bytes=64)
+        weighed = small("weighed")
+        weigh(weighed, target_part[second][:], rest)
+        draft_part[third] = small("draft_third")
+        weigh(draft_part[third], fetched[third][:], share)
+        nc.vector.tensor_tensor(mixed[second][:], weighed[:], draft_part[second][:], ADD)
+        weave(first, 0, FIRST_VECTOR, nc.vector.tensor_copy)
         put_back(second)
+
         target_plane(third, 0)
+        gap_plane(last, keep.tile([P, S], F32, name="gap_last", align_bytes=64))
         fetch_target(third)
-        mix_on_gpsimd(third, target_part[third], rest, draft_part[third], small("weighed"))
-        put_back(third)
-        gap_plane(last, f"target{second}")
-        target_plane(last, 0)
+        target_plane(last, 2)
         fetch(fetched[last], gap[last])
+        mixed[third] = small("weighed")
+        nc.gpsimd.tensor_tensor(mixed[third][:], draft_part[third][:], target_part[third][:], ADD)
+        put_back(third)
+        draft_part[last] = small("woven_right")
+        nc.gpsimd.tensor_tensor(draft_part[last][:], fetched[last][:], share[:], MULT)
+        weave(first, FIRST_VECTOR, half, nc.scalar.copy)
         fetch_target(last)
-        mix_on_gpsimd(last, fetched[last], share, target_part[last], small("woven_right"))
+        mixed[last] = small("mixed_last")
+        nc.gpsimd.tensor_tensor(mixed[last][:], draft_part[last][:], target_part[last][:], ADD)
         put_back(last)
         woven.append(keep.tile([P, half, PACK], BF16, name="woven_right", align_bytes=64))
         weave(second, 0, half, nc.scalar.copy)
         weave(first, half, S, nc.scalar.copy)
         weave(third, 0, half, nc.scalar.copy)
         for t in (second, third):
-            weave(t, MIDDLE_SCALAR, S, round_on_gpsimd)
-        for t in (second, third):
-            weave(t, half, MIDDLE_SCALAR, nc.scalar.copy)
+            weave(t, half, S, round_on_gpsimd)
         for c0, c1 in OUT_PIECES:
             weave(last, c0, c1, nc.vector.tensor_copy if c1 <= half else nc.scalar.copy)
 

from contextlib import ExitStack

import concourse.mybir as mybir

K, T, S, V, N = 512, 2048, 512, 256, 512
FLOPS = 2 * 2 * K * N * S

F32 = mybir.dt.float32
BF16 = mybir.dt.bfloat16
I32 = mybir.dt.int32
U32 = mybir.dt.uint32
U16 = mybir.dt.uint16
U8 = mybir.dt.uint8
FP8X4 = mybir.dt.float8_e4m3fn_x4
MULT = mybir.AluOpType.mult
ADD = mybir.AluOpType.add
COPY = mybir.ActivationFunctionType.Copy

P = 128
PACK = 4
QUADRANT = 32
LIST_ROWS = 16
PLANE_BYTES = 4 * S

ORDER = (0, 2, 3, 1)

W2_VECTOR = 336
W1_VECTOR = (512, 288)
FIRST_PLANE_PIECES = ((0, 0, 256), (1, 256, 384), (2, 384, 512))
FIRST_VECTOR = 128
OUT_PIECES = ((0, 128), (128, 256), (256, 384), (384, 512))


def tile_picked_specacc_none_po_kernel(
    tc, x_words, x_scales, w1, w2, sh, offs, acc_l, out_0, out_1, out_2
):
    nc = tc.nc
    with ExitStack() as ctx:
        keep = ctx.enter_context(tc.tile_pool(name="keep", bufs=1))
        psum = ctx.enter_context(tc.psum_pool(name="psum", bufs=1))
        stage = ctx.enter_context(tc.tile_pool(name="stage", bufs=1))
        late = ctx.enter_context(tc.tile_pool(name="late", bufs=1))

        scale_table = keep.tile([P, T], U8, name="scale_table")
        nc.vector.memset(scale_table[:, : T // 2].bitcast(I32), 0)
        nc.gpsimd.memset(scale_table[:, T // 2 :].bitcast(I32), 0)

        raw2 = keep.tile([P, PACK, N], F32, name="raw2")
        nc.sync.dma_start(raw2[:], w2.rearrange("(p j) c -> p j c", j=PACK))
        picks = keep.tile([P, S // LIST_ROWS], U16, name="picks")
        nc.sync.dma_start(picks[:], offs)
        for r in range(PACK):
            nc.sync.dma_start(scale_table[r:P:QUADRANT, :].bitcast(I32), x_scales[0, r:16:PACK, :].bitcast(I32))
        word_table = keep.tile([P, T], U32, name="word_table", align_bytes=64)
        nc.sync.dma_start(word_table[:].bitcast(I32), x_words[0].rearrange("p n t -> p (n t)").bitcast(I32))
        raw1 = stage.tile([P, PACK, N], F32, name="raw1", offset=0, align_bytes=64)
        nc.sync.dma_start(raw1[:], w1.rearrange("(p j) c -> p j c", j=PACK))
        accepted = keep.tile([P, V // LIST_ROWS], U16, name="accepted")
        nc.sync.dma_start(accepted[:], acc_l)
        share = keep.tile([P, V], F32, name="share")
        nc.sync.dma_start(share[:], sh.rearrange("(p t) v -> p t v", t=PACK)[:, 0, :])

        def negate_on_scalar(dest, src):
            nc.scalar.activation(dest, src, COPY, scale=-1.0)

        def negate_on_vector(dest, src):
            nc.vector.tensor_scalar(dest, src, -1.0, None, MULT)

        def round_pair(grouped, raw, t0, c0, c1, copy):
            copy(
                grouped[:, :, c0 // PACK : c1 // PACK, :].rearrange("p t m j -> p m j t"),
                raw[:, :, c0:c1].rearrange("p j (m t) -> p m j t", t=PACK)[:, :, :, t0 : t0 + 2],
            )

        def quantise_pair(grouped, name, slot=None):
            codes = keep.tile([P, 2 * P], U32, name=slot or f"codes_{name}", align_bytes=64)
            scales = keep.tile([P, 2 * P], U8, name=f"scales_{name}", align_bytes=64)
            nc.vector.quantize_mx(
                out=codes[:].bitcast(FP8X4), scales=scales[:], in_=grouped.rearrange("p t m j -> p (t m j)")
            )
            return [(codes[:, i * P : (i + 1) * P], scales[:, i * P : (i + 1) * P]) for i in range(2)]

        def mx_pass(bank, operand, c0, c1, start, stop):
            codes, scales = operand
            nc.tensor.matmul_mx(
                out=bank,
                lhsT=codes.bitcast(FP8X4),
                lhsT_scale=scales,
                rhs=x_codes[:, c0:c1].bitcast(FP8X4),
                rhs_scale=x_scale[:, c0:c1],
                start=start,
                stop=stop,
            )

        def product(operand, dest, bank_no, c0, c1, copy):
            bank = psum.tile([P, c1 - c0], F32, name=f"bank{bank_no}")
            mx_pass(bank[:], operand, c0, c1, True, True)
            copy(dest[:, c0:c1], bank[:])

        def fetch(picked, plane):
            nc.scalar.activation(picked[:], plane[:].indirect(accepted[:]), COPY)

        def weigh(weighed, values, weights):
            nc.vector.tensor_tensor(weighed[:], values, weights[:], MULT)

        def small(name):
            return keep.tile([P, V], F32, name=name, align_bytes=64)

        x_scale = keep.tile([P, S], U8, name="x_scale", align_bytes=64)
        nc.vector.tensor_copy(x_scale[:], scale_table[:].indirect(picks[:]))
        grouped2 = [keep.tile([P, 2, P, PACK], BF16, name=f"grouped2_{pair}", align_bytes=64) for pair in range(2)]
        round_pair(grouped2[0], raw2, 0, 0, W2_VECTOR, negate_on_vector)
        round_pair(grouped2[0], raw2, 0, W2_VECTOR, N, negate_on_scalar)
        round_pair(grouped2[1], raw2, 2, 0, N, negate_on_scalar)
        draft_weights = quantise_pair(grouped2[0][:], "w2a")
        x_codes = keep.tile([P, S], U32, name="x_codes", align_bytes=64)
        half, half_list = S // 2, S // 2 // LIST_ROWS
        for h in range(2):
            offsets = picks[:, h * half_list : (h + 1) * half_list]
            nc.vector.tensor_copy(x_codes[:, h * half : (h + 1) * half], word_table[:].indirect(offsets))

        draft_weights = draft_weights + quantise_pair(grouped2[1][:], "w2b", "word_table")

        first, second, third, last = ORDER
        e = {first: keep.tile([P, S], F32, name="e_first"), second: stage.tile([P, S], F32, name="e_second", offset=0)}
        gap_banks = {t: psum.tile([P, S], F32, name=f"bank{bank_no}") for t, bank_no in ((third, 4), (last, 5))}
        for bank_no, c0, c1 in FIRST_PLANE_PIECES:
            product(draft_weights[first], e[first], bank_no, c0, c1, negate_on_scalar)
            if c1 % half == 0:
                mx_pass(gap_banks[last][:, c1 - half : c1], draft_weights[last], c1 - half, c1, c1 == half, False)
        second_bank = psum.tile([P, S], F32, name="bank3")
        mx_pass(second_bank[:], draft_weights[second], 0, S, True, True)
        mx_pass(gap_banks[third][:], draft_weights[third], 0, S, True, False)

        raw1_bytes = PACK * PLANE_BYTES
        grouped1 = []
        for pair, split in enumerate(W1_VECTOR):
            grouped1.append(
                stage.tile([P, 2, P, PACK], BF16, name=f"grouped1_{pair}", offset=raw1_bytes + pair * PLANE_BYTES)
            )
            round_pair(grouped1[pair], raw1, 2 * pair, 0, split, nc.vector.tensor_copy)
            if split < N:
                round_pair(grouped1[pair], raw1, 2 * pair, split, N, nc.scalar.copy)
        target_weights = quantise_pair(grouped1[0][:], "w1a") + quantise_pair(grouped1[1][:], "w1b")

        fetched_e = small("fetched_e")
        fetch(fetched_e, e[first])
        negate_on_scalar(e[second][:], second_bank[:])
        rest = stage.tile([P, V], F32, name="rest", offset=raw1_bytes + PLANE_BYTES // 2)
        nc.vector.tensor_scalar(rest[:], share[:], -1.0, 1.0, MULT, ADD)
        draft_part = {
            second: small("draft_second"),
            first: stage.tile([P, V], F32, name="draft_first", offset=raw1_bytes),
        }
        weigh(draft_part[first], fetched_e[:], share)
        weigh(draft_part[second], e[second][:].indirect(accepted[:]), share)

        out, gap, target_part, fetched, mixed = {}, {}, {}, {}, {}
        out_rows = out_0.rearrange("(p t) c -> p t c", t=PACK)

        def target_plane(t, bank_no):
            out[t] = keep.tile([P, S], F32, name=f"out{t}", align_bytes=64)
            product(target_weights[t], out[t], bank_no, 0, S, nc.scalar.copy)

        def gap_plane(t, tile):
            gap[t] = tile
            mx_pass(gap_banks[t][:], target_weights[t], 0, S, False, True)
            negate_on_scalar(gap[t][:], gap_banks[t][:])
            fetched[t] = small(f"fetched{t}")

        def fetch_target(t):
            target_part[t] = small(f"target{t}")
            fetch(target_part[t], out[t])

        def put_back(t):
            nc.vector.tensor_copy(out[t][:].indirect(accepted[:]), mixed[t][:])
            nc.sync.dma_start(out_rows[:, t, :], out[t][:])

        def round_on_gpsimd(dest, src):
            nc.gpsimd.tensor_scalar(dest, src, 1.0, 0.0, MULT, ADD)

        def weave(t, c0, c1, copy):
            h = c0 // half
            copy(woven[h][:, c0 - h * half : c1 - h * half, t], out[t][:, c0:c1])

        out[first] = keep.tile([P, S], F32, name="out_first", align_bytes=64)
        product(target_weights[first], out[first], 6, 0, half, nc.scalar.copy)
        product(target_weights[first], out[first], 1, half, S, nc.scalar.copy)
        target_part[first] = small("target_first")
        weigh(target_part[first], out[first][:].indirect(accepted[:]), rest)
        nc.vector.tensor_tensor(out[first][:].indirect(accepted[:]), target_part[first][:], draft_part[first][:], ADD)
        nc.sync.dma_start(out_rows[:, first, :], out[first][:])

        target_plane(second, 7)
        gap_plane(third, late.tile([P, S], F32, name="gap_third", offset=PLANE_BYTES // 2, align_bytes=64))
        fetch_target(second)
        fetch(fetched[third], gap[third])
        woven = [late.tile([P, half, PACK], BF16, name="woven_left", offset=0, align_bytes=64)]
        mixed[second] = late.tile([P, V], F32, name="mixed_second", offset=PLANE_BYTES, align_bytes=64)
        weighed = small("weighed")
        weigh(weighed, target_part[second][:], rest)
        draft_part[third] = small("draft_third")
        weigh(draft_part[third], fetched[third][:], share)
        nc.vector.tensor_tensor(mixed[second][:], weighed[:], draft_part[second][:], ADD)
        weave(first, 0, FIRST_VECTOR, nc.vector.tensor_copy)
        put_back(second)

        target_plane(third, 0)
        gap_plane(last, keep.tile([P, S], F32, name="gap_last", align_bytes=64))
        fetch_target(third)
        target_plane(last, 2)
        fetch(fetched[last], gap[last])
        mixed[third] = small("weighed")
        nc.gpsimd.tensor_tensor(mixed[third][:], draft_part[third][:], target_part[third][:], ADD)
        put_back(third)
        draft_part[last] = small("woven_right")
        nc.gpsimd.tensor_tensor(draft_part[last][:], fetched[last][:], share[:], MULT)
        weave(first, FIRST_VECTOR, half, nc.scalar.copy)
        fetch_target(last)
        mixed[last] = small("mixed_last")
        nc.gpsimd.tensor_tensor(mixed[last][:], draft_part[last][:], target_part[last][:], ADD)
        put_back(last)
        woven.append(keep.tile([P, half, PACK], BF16, name="woven_right", align_bytes=64))
        weave(second, 0, half, nc.scalar.copy)
        weave(first, half, S, nc.scalar.copy)
        weave(third, 0, half, nc.scalar.copy)
        for t in (second, third):
            weave(t, half, S, round_on_gpsimd)
        for c0, c1 in OUT_PIECES:
            weave(last, c0, c1, nc.vector.tensor_copy if c1 <= half else nc.scalar.copy)

        out_scales = keep.tile([P, S], U8, name="out_scales", align_bytes=64)
        out_words = out_1[0].rearrange("p c t -> p (c t)").bitcast(I32)
        out_codes = keep.tile([P, S], U32, name="out_codes", align_bytes=64)
        for c0, c1 in OUT_PIECES:
            nc.vector.quantize_mx(
                out=out_codes[:, c0:c1].bitcast(FP8X4),
                scales=out_scales[:, c0:c1],
                in_=woven[c0 // half][:, c0 % half : c0 % half + c1 - c0, :].rearrange("p c t -> p (c t)"),
            )
            if c1 % half == 0:
                nc.sync.dma_start(out_words[:, c1 - half : c1], out_codes[:, c1 - half : c1].bitcast(I32))
        for q in range(P // QUADRANT):
            queue = nc.scalar if q % 2 == 0 else nc.sync
            queue.dma_start(
                out_2[0, PACK * q : PACK * (q + 1), :].bitcast(I32),
                out_scales[QUADRANT * q : QUADRANT * q + PACK, :].bitcast(I32),
            )
